import numpy as np, ml_dtypes
CORES = [40,64,80,88,96,104,120,144]
N = 8
import mx_ref
BF = ml_dtypes.bfloat16
def gentries(a):
    return np.ascontiguousarray(a.reshape(8, 16, -1).transpose(0, 2, 1)).reshape(8, -1)
def gtable(e):
    e = np.asarray(e); return np.ascontiguousarray(e.reshape(8, -1, 16).transpose(0, 2, 1)).reshape(128, -1).astype(np.int32)
def gcols(t, e):
    v = np.concatenate([t.reshape(8, 16, -1, 4), np.zeros((8, 16, 1, 4), BF)], axis=2)
    return np.ascontiguousarray(np.stack([v[g][:, e[g]] for g in range(8)])).reshape(128, -1)
def tile(rs):
    return np.stack(rs, axis=2).reshape(128, -1).astype(BF)
def pick(q, e):
    c = np.concatenate([q[0].reshape(128, -1, 4), np.zeros((128, 1, 4), np.uint8)], axis=1); s = np.concatenate([q[1], np.ones((16, 1), np.uint8)], axis=1)
    return (np.ascontiguousarray(c[:, e].reshape(128, -1)), np.ascontiguousarray(s[:, e]))
def join(*qs):
    return (np.concatenate([q[0] for q in qs], axis=1), np.concatenate([q[1] for q in qs], axis=1))
def put(q, e, v):
    c, s = q[0].reshape(128, -1, 4).copy(), q[1].copy(); c[:, e] = v[0].reshape(128, -1, 4); s[:, e] = v[1]
    return (c.reshape(128, -1), s)
def pk(c, s):
    return (np.ascontiguousarray(c), mx_ref.live(s))
def emit(q):
    return q[0], q[1]
def packed(v, rng):
    q = [mx_ref.quantize(np.ascontiguousarray(v[r])) for r in range(N)]
    return np.stack([a for a, b in q]), np.stack([mx_ref.plane(b, rng) for a, b in q])
def values_of_codes():
    e, c = np.zeros((128, 128, 4), np.float32), np.zeros((128, 2, 4), np.uint8)
    e[np.arange(128), np.arange(128), 0] = 1
    c[:127, :, 0] = np.arange(256).reshape(2, 128).T[:127]
    return mx_ref.matmul(mx_ref.quantize(e.reshape(128, 512).astype(BF)), (c.reshape(128, 8), np.full((16, 2), 127, np.uint8))).T.reshape(-1).astype(np.float64)
CODE_VALUE, SCALE_VALUE = values_of_codes(), 2.0 ** (np.arange(256) - 127.0)
def decode(q):
    return (CODE_VALUE[q[0]].reshape(16, 8, -1, 4) * SCALE_VALUE[q[1]][:, None, :, None] + 0.0).reshape(128, -1).astype(np.float32)
def f(rng, *shape):
    return mx_ref.flush((rng.standard_normal(shape, dtype=np.float32) * np.exp2(rng.integers(-2, 3, shape[:-1] + (1,)))).astype(BF))
def wide(rng, *shape, cols=0):
    v = rng.standard_normal(shape, dtype=np.float32) * np.exp2(rng.integers(-12, 13, shape)).astype(np.float32)
    if cols: v *= np.repeat(np.exp2(rng.integers(-cols, cols + 1, shape[:-2] + (1, shape[-1] // 4))) * (rng.random(shape[:-2] + (1, shape[-1] // 4)) > 0.0625), 4, axis=-1).astype(np.float32)
    return mx_ref.flush(v.astype(BF))
C, H = 288, 144
STEP = [4, 1, 2]
def numbers_of(rng):
    return {"x": np.array(f(rng, N, 128, 4 * C)), "u": np.array(f(rng, N, 128, 512)), "v": np.array(f(rng, N, 128, 512))}
def stored(m):
    return {"ml": np.stack([gtable(m[r]) for r in range(N)])}
def paired(e):
    m = np.zeros_like(e)
    np.put_along_axis(m, e, np.roll(e, H, axis=-1), axis=-1)
    return m
def pairings(rng):
    return paired(rng.permuted(np.tile(np.arange(C), (N, 8, 1)), axis=2))
def zigzag(rng, loop):
    s, t = rng.permutation(H), rng.permutation(H)
    a = np.concatenate([np.roll(t, -1), H + np.roll(s, -1)]).reshape(-1, 2)
    if not loop: a[H // 2 - 1, 1], a[-1, 0] = int(a[-1, 0]), int(a[H // 2 - 1, 1])
    b = np.concatenate([s, H + t]).reshape(-1, 2)
    return [paired(np.concatenate([k[:, 0], k[:, 1]])) for k in (a, b)]
def coil(rng):
    s = rng.permutation(H)
    k = np.concatenate([s, H + np.roll(s[:-1], -1), H + s[-1:]]).reshape(-1, 2)
    k[H // 2 - 1, 1], k[-1, 0] = int(k[-1, 0]), int(k[H // 2 - 1, 1])
    return paired(np.concatenate([k[:, 0], k[:, 1]]))
def layers(rng, still=[], pairs=False):
    w = np.array(f(rng, N, 128, 2048)).reshape(N, 8, 16, 4, 8, 16, 4)
    for i in still:
        w[:, :, i] = 0
        w[:, :, :, :, :, i] = 0
    if pairs:
        w[:, :, :, :, :, 8:] = 0
        for g in range(8):
            w[:, g, 8, 0, g, 8, 0] = -28.0
            for b in range(4): w[:, g, 10, b, g, 9, 0] = -2.0 ** (b - 5)
    return w
def weights(rng, w):
    c, s = packed(np.ascontiguousarray(w).reshape(N, 128, 2048), rng)
    return {"wc": c, "ws": s}
def setup_inputs(rng):
    return {**numbers_of(rng), **stored(pairings(rng)), **weights(rng, layers(rng))}
def setup_inputs_ties(rng):
    d = numbers_of(rng)
    o = rng.permutation(N)
    k = rng.integers(0, 4, (N, 8, C))
    k[o[0]] = 0
    k[o[1]] -= 4
    k[o[2]] = np.arange(C) < H
    kind = rng.permutation(8)
    m = np.zeros((N, 8, C), np.int64)
    for g in range(8):
        if 4 <= kind[g] < 7: k[:, g] = np.sort(k[:, g].reshape(N, 2, H), axis=1).reshape(N, C)
        for r in range(N):
            p, q = r ^ STEP[0], r ^ STEP[1]
            if kind[g] < 4 and r < p:
                a = zigzag(rng, kind[g] == 3)
                j = int(rng.integers(2))
                m[r, g], m[p, g] = a[j], a[1 - j]
            if 4 <= kind[g] < 6 and r < min(p, q, p ^ STEP[1]):
                m[r, g], m[q, g] = zigzag(rng, False)
                m[p, g] = m[p ^ STEP[1], g] = paired(np.arange(C))
            if kind[g] == 7: m[r, g] = paired(np.concatenate([rng.permutation(H), H + rng.permutation(H)]))
        if kind[g] == 6:
            m[:, g] = paired(np.arange(C))
            r = int(rng.integers(N))
            if STEP[0] ^ STEP[1] == STEP[2]: m[r, g] = coil(rng)
            else: m[r, g], m[r ^ STEP[2], g] = zigzag(rng, False)
    x = d["x"].reshape(N, 8, 16, C, 4)
    x[:, :, 0] = 0
    x[:, :, 0, :, 0] = k.astype(np.float32).astype(BF)
    a = np.exp2(rng.integers(-3, 4, (N, 8, 1)).astype(np.float32))
    x[:, :, 8:] = 0
    x[:, :, 8, :, 0] = (-1.125 * a).astype(BF)
    x[:, :, 10, :, 0] = (-0.0703125 * a).astype(BF)
    u = d["u"].reshape(N, 128, 128, 4)
    u[:, :, ::16] = 0
    for h in range(0, 128, 16): u[:, h, h, 0] = 1.0
    return {"x": x.reshape(N, 128, 4 * C), "u": u.reshape(N, 128, 512), "v": d["v"], **stored(twist(k, m)), **weights(rng, layers(rng, [0], True))}
def setup_inputs_near(rng):
    d = numbers_of(rng)
    x = d["x"].astype(np.float32).reshape(N, 8, 16, C, 4)
    x[:, :, 0] = 0
    x[:, :, 8:] = 0
    u = d["u"].reshape(N, 128, 128, 4)
    u[:, :, ::16] = 0
    w = layers(rng, [0, 8, 9, 10, 11, 12, 13, 14, 15])
    o = rng.permutation(N) % 4
    for r in range(N):
        c = rng.choice([-1.0, 1.0], (8, 1))
        s = rng.integers(0, 16, (8, C))
        digits = ((s[:, :, None] >> np.arange(4)) & 1) * np.exp2(np.arange(4) - 23.0)
        if o[r] < 2:
            x[r, :, 0, :, 0] = c
            x[r, :, 8] = digits
            x[r, :, 11, :, 0] = 2.0 ** -10
        elif o[r] == 2: x[r, :, 8] = digits * rng.choice([-1.0, 1.0], (8, C, 1))
        else:
            x[r, :, 8, :, 0] = np.where(s < 8, 1.25, 0.0) * 2.0 ** -30 * c
            x[r, :, 9, :, 0] = np.where(s < 8, 0.0, 1.125) * 2.0 ** -30 * c
            for g in rng.permutation(8)[:4]:
                e = rng.choice([-1.0, 1.0], C) * 2.0 ** -30
                x[r, g, 8, :, 0] = 1.25 * e
                x[r, g, 9, :, 0] = -1.125 * e
            for g in range(8):
                w[r, g, 8, 0, g, 12, 0] = 2.0 ** -8
                w[r, g, 8, 0, g, 14, 0] = 64.0
                w[r, g, 1, 0, g, 2, 0] = 256.0
        at = [0, C - 1, int(rng.integers(C)), int(rng.integers(C))]
        for g, j in zip(rng.permutation(8)[:4], at): x[r, g, 0, j, 0] = 2.0 ** 29 * rng.choice([-1.0, 1.0])
        k = 1.0 if o[r] == 0 else 2.0 ** -30
        for h in range(0, 128, 16):
            u[r, h, h, 0] = k if o[r] < 2 else 1.0
            if o[r] < 2: u[r, h + 11, h, 0] = k
            if o[r] < 3: u[r, h + 8, h] = k
            else:
                u[r, h + 8, h, 0] = k
                u[r, h + 9, h, 0] = 1.125 * k
                u[r, h + 12, h, 0] = k
    return {"x": x.reshape(N, 128, 4 * C).astype(BF), "u": u.reshape(N, 128, 512), "v": d["v"], **stored(pairings(rng)), **weights(rng, w)}
def setup_inputs_odd(rng):
    d = numbers_of(rng)
    x = (1.0 + (2 * rng.integers(0, 64, (N, 16, 8, C, 4)) + 1) * 2.0 ** -7) * np.exp2(-rng.integers(0, 7, (N, 16, 8, C, 4)).astype(np.float64)) * rng.choice([-1.0, 1.0], (N, 16, 8, C, 4))
    x[:, :, 0, :, 0] = 1.96875 * 2.0 ** 8 * rng.choice([-1.0, 1.0], (N, 16, C))
    u = d["u"].reshape(N, 16, 8, 128, 4)
    u[:, :, 0, ::16] = 0
    for r in range(N):
        for i, g in enumerate(rng.permutation(8)[:4]):
            x[r, 2 * g, 1, :, 0] = (8 + rng.integers(0, 2, C)) * 2.0 ** (i - 8)
            u[r, :, :, 16 * g] = 0
            u[r, 2 * g, 1, 16 * g, 0] = 1.0
    return {"x": x.astype(np.float32).reshape(N, 128, 4 * C).astype(BF), "u": u.reshape(N, 128, 512), "v": d["v"], **stored(pairings(rng)), **weights(rng, layers(rng, [0, 8]))}
def setup_inputs_ends(rng):
    d = numbers_of(rng)
    x = np.zeros((N, 8, 16, C, 4))
    u = d["u"].astype(np.float32).reshape(N, 128, 128, 4)
    v = d["v"].astype(np.float32)
    w = np.zeros((N, 128, 4, 128, 4), np.float32)
    m = pairings(rng)
    o, e = rng.permutation(N) % 4, rng.permutation(N) % 4
    i = np.arange(128)
    for r in range(N):
        h = rng.permutation(8)
        c = np.where(h < 2, 0.0, h % 2 * 2.0 - 1.0)[None, :, None]
        k = np.array([2.0, 4.0, -4.0])[rng.permutation(8) % 3]
        low = -(0.9 + 0.1 * rng.random((8, 16, C, 4))) * 2.0 ** 28
        if o[r] == 0: x[r] = low
        if o[r] == 1: x[r] = low * rng.choice([-1.0, 1.0], (C, 1))
        if o[r] < 2:
            u[r, :, ::16] = c * (0.9 + 0.1 * rng.random((128, 8, 4))) * 2.0 ** 30
            v[r] = rng.choice([-1.0, 1.0], (128, 512)) * (0.9 + 0.1 * rng.random((128, 512))) * 2.0 ** 30
        if o[r] == 2:
            x[r] = -(1.0 + 0.125 * rng.integers(0, 8, (8, 16, C, 4))) * 2.0 ** -30
            u[r, :, ::16] = c * (1.0 + 0.125 * rng.integers(0, 8, (128, 8, 4))) * 2.0 ** -30
            v[r] = rng.choice([-1.0, 1.0], (128, 512)) * (1.0 + 0.125 * rng.integers(0, 8, (128, 512))) * 2.0 ** -30
            k[:] = 32.0
        if o[r] == 3:
            x[r] = d["x"][r].astype(np.float32).reshape(8, 16, C, 4)[:, :, :1]
            u[r, :, ::16] *= np.abs(c).astype(np.float32)
        for b in range(4): w[r, i, b, i, b] = k[i // 16]
        if e[r] < 3: m[r] = [paired(np.arange(C)), np.arange(C) ^ 1, C - 1 - np.arange(C)][e[r]]
    return {"x": x.astype(np.float32).reshape(N, 128, 4 * C).astype(BF), "u": u.reshape(N, 128, 512).astype(BF), "v": v.astype(BF), **stored(m), **weights(rng, w.astype(BF))}
def setup_inputs_spread(rng):
    d = setup_inputs(rng)
    d["x"] = wide(rng, N, 128, 4 * C, cols=6)
    return d
def check_inputs(d):
    b = []
    for k in ("x", "u", "v"):
        a = np.abs(d[k].astype(np.float32))
        if not (np.isfinite(a).all() and ((a == 0) | (a >= 2.0 ** -30) & (a <= 2.0 ** 30)).all()): b.append("a value of " + k)
    none, least, most = [emit(mx_ref.quantize(np.full((128, 16), k, np.float32).astype(BF)))[1][0, 0] for k in (0.0, 2.0 ** -8, 2.0 ** 8)]
    for r in range(N):
        e = gentries(d["ml"][r]).astype(np.int64)
        if not ((e >= 0) & (e < C)).all(): b.append("an entry of ml")
        elif (e == np.arange(C)).any() or (np.take_along_axis(e, e, axis=1) != np.arange(C)).any(): b.append("ml: not a pairing")
        if ((d["wc"][r] == 0x7F) | (d["wc"][r] == 0xFF)).any(): b.append("wc: a code that is no number")
        s = mx_ref.live(d["ws"][r])
        if ((s != none) & ((s < least) | (s > most))).any(): b.append("ws: a scale out of range")
    return b
def twist(s, m):
    e = np.zeros(m.shape, np.int64) + np.arange(C)
    swap = H * (s[..., :H] > s[..., H:])
    e[..., :H] += swap
    e[..., H:] -= swap
    return np.take_along_axis(e, np.take_along_axis(m, e, axis=-1), axis=-1)
def glued(a, b):
    at = np.tile(np.arange(C), (8, 1))
    far = at >= H
    done = np.zeros((8, C), bool)
    for _ in range(H + 1):
        at = np.where(done, at, np.where(far, np.take_along_axis(b, at, axis=1), np.take_along_axis(a, at, axis=1)))
        done = done | ((at >= H) == far)
        at = np.where(done, at, np.where(far, at + H, at - H))
        far = far ^ ~done
        if done.all(): break
    return at
def plus(s, t):
    return (s.astype(np.float32) + t.astype(np.float32)).astype(BF)
def reference(x, u, v, ml, wc, ws):
    qu = [mx_ref.quantize(u[r]) for r in range(N)]
    lay = [pk(wc[r], ws[r]) for r in range(N)]
    now = [x[r] for r in range(N)]
    mate = [gentries(ml[r]).astype(np.int64) for r in range(N)]
    for step in STEP:
        turned, qa = [], []
        for r in range(N):
            s = mx_ref.matmul(qu[r], mx_ref.quantize(now[r]))[::16] + np.float32(0.0)
            turned.append(twist(s, mate[r]))
            qz = mx_ref.quantize(plus(now[r], gcols(now[r], turned[r])))
            qa.append(mx_ref.quantize(tile([mx_ref.matmul(pick(lay[r], np.arange(128 * b, 128 * b + 128)), qz) * np.float32(0.015625) for b in range(4)])))
        made = []
        for r in range(N):
            p = r ^ step
            mate[r] = glued(turned[r], turned[p])
            t = decode(join(pick(qa[r], np.arange(H)), pick(qa[p], np.arange(H, C)))).astype(BF)
            made.append(plus(now[r], gcols(t, mate[r])))
        now = made
    y, mo = np.zeros((N, 128, C), np.float32), np.zeros((N, 8, C), np.float32)
    oc, osc = np.zeros((N, 128, 4 * C), np.uint8), np.zeros((N, 16, C), np.uint8)
    for r in range(N):
        q = mx_ref.quantize(now[r])
        y[r] = mx_ref.matmul(mx_ref.quantize(v[r]), q)
        mo[r] = mate[r]
        oc[r], osc[r] = emit(q)
    return {"y": y, "mo": mo, "oc": oc, "osc": osc}

@@ -1,0 +1,467 @@
+from concourse.bass import DstId, RemoteDMATransfer
+from concourse.mybir import dt, AluOpType, ActivationFunctionType
+
+C, H = 288, 144
+STEP = (4, 1, 2)
+AW, MID = 432, 216
+ROUNDS = len(STEP)
+
+SCRATCH = {}
+for _n in ("x0", "x1", "x2", "x3", "z", "a"):
+    SCRATCH[_n] = ("sbuf", [128, 4 * C], "bfloat16")
+for _n in ["x", "z"] + ["a%d" % i for i in range(ROUNDS)]:
+    SCRATCH["q" + _n] = ("sbuf", [128, C], "float8_e4m3fn_x4")
+    SCRATCH["s" + _n] = ("sbuf", [128, C], "uint8")
+for _n in range(ROUNDS):
+    SCRATCH["qp%d" % _n] = ("sbuf", [128, H], "float8_e4m3fn_x4")
+    SCRATCH["sp%d" % _n] = ("sbuf", [128, H], "uint8")
+    SCRATCH["lu%d" % _n] = ("sbuf", [128, 10], "uint16")
+    SCRATCH["ll%d" % _n] = ("sbuf", [128, 10], "uint16")
+    SCRATCH["na%d" % _n] = ("sbuf", [128, 20], "uint16")
+for _n in ("u", "v"):
+    SCRATCH[_n + "t"] = ("sbuf", [128, 512], "bfloat16")
+for _n in ("u", "r", "v"):
+    SCRATCH["q" + _n] = ("sbuf", [128, 128], "float8_e4m3fn_x4")
+    SCRATCH["s" + _n] = ("sbuf", [128, 128], "uint8")
+for _n in ("w", "e"):
+    SCRATCH["q" + _n] = ("sbuf", [128, 512], "float8_e4m3fn_x4")
+    SCRATCH["s" + _n] = ("sbuf", [128, 512], "uint8")
+SCRATCH.update({
+    "et": ("sbuf", [128, 2048], "bfloat16"),
+    "ones": ("sbuf", [128, 128], "bfloat16"),
+    "idn": ("sbuf", [128, 128], "bfloat16"),
+    "mli": ("sbuf", [128, 18], "int32"),
+    "mlf": ("sbuf", [128, 20], "float32"),
+    "mlg": ("sbuf", [128, 20], "float32"),
+    "mlh": ("sbuf", [128, 20], "float32"),
+    "mli2": ("sbuf", [128, 20], "float32"),
+    "lm": ("sbuf", [128, 28], "uint16"),
+    "mm": ("sbuf", [128, 20], "float32"),
+    "mt": ("sbuf", [128, 20], "float32"),
+    "w1": ("sbuf", [128, 20], "float32"),
+    "d1": ("sbuf", [128, 10], "float32"),
+    "e1": ("sbuf", [128, 10], "float32"),
+    "nn": ("sbuf", [128, 20], "float32"),
+    "xp": ("sbuf", [128, 4 * C], "bfloat16"),
+    "fl": ("sbuf", [128, AW], "bfloat16"),
+    "scu": ("sbuf", [128, H], "float32"),
+    "mgt": ("sbuf", [128, 448], "bfloat16"),
+    "sct": ("sbuf", [128, 448], "bfloat16"),
+    "mskt": ("sbuf", [128, 448], "bfloat16"),
+    "rst": ("sbuf", [128, 448], "bfloat16"),
+    "msk": ("sbuf", [128, 304], "bfloat16"),
+    "mg": ("sbuf", [128, 304], "bfloat16"),
+    "sc": ("sbuf", [128, 304], "bfloat16"),
+    "h": ("sbuf", [128, C], "bfloat16"),
+    "up": ("sbuf", [128, C], "bfloat16"),
+    "vtab": ("sbuf", [128, C], "bfloat16"),
+    "ta": ("sbuf", [128, AW], "bfloat16"),
+    "tb": ("sbuf", [128, AW], "bfloat16"),
+    "tc": ("sbuf", [128, AW], "bfloat16"),
+    "gtb": ("sbuf", [128, AW], "float32"),
+    "lk0": ("sbuf", [128, 10], "uint16"),
+    "lk1": ("sbuf", [128, 10], "uint16"),
+    "db": ("sbuf", [128, 4 * AW], "bfloat16"),
+    "mrow": ("sbuf", [128, 304], "float32"),
+    "ys": ("sbuf", [128, C], "float32"),
+    "iom": ("sbuf", [128, 448], "int32"),
+    "ioa": ("sbuf", [128, 448], "int32"),
+    "ul": ("sbuf", [128, 8], "int32"),
+    "uo": ("sbuf", [128, 8], "uint16"),
+    "pc": ("sbuf", [128, 9], "int32"),
+    "pd": ("sbuf", [128, 9], "int32"),
+    "k16": ("sbuf", [128, 9], "int32"),
+    "idl": ("sbuf", [128, 9], "int32"),
+    "ps": ("psum", [128, 4096], "float32"),
+})
+LOADS = ["ldxu", "ldxl", "ldu", "ldm", "ldw", "lds", "ldv"]
+STORES = ["sty0", "sty1", "stc0", "stc1", "sts0", "sts1", "sts2", "sts3", "stm0", "stm1"]
+SEMAPHORES = (["ve", "ac", "pe", "gp", "out"] + LOADS + STORES
+              + [n + "%d" % i for n in ("lu", "ll", "qp", "sp") for i in range(ROUNDS)])
+
+
+def relays(topo, src, dst):
+    ks = [k for k in topo.cores_of(src) if k != src and topo.may_write(k, dst)]
+    return sorted(ks, key=lambda k: (topo.die(k) != topo.die(src), k))[:2]
+
+
+def bits(es):
+    return sum(1 << e for e in es)
+
+
+def chip_masks(topo, src, rl):
+    e = topo.engines(src, rl[0])
+    f = topo.engines(src, rl[1])
+    n = len(e) // 2
+    return [e[:n], [k for k in f if k not in e[:n]][:n]]
+
+
+def relay_program(g, core, T, topo):
+    home = [r for r, c in enumerate(T.cores) if core in topo.cores_of(c)]
+    if not home:
+        return
+    r = home[0]
+    src = T.cores[r]
+    sent = 0
+    for i, s in enumerate(STEP):
+        dst = T.cores[r ^ s]
+        rl = relays(topo, src, dst)
+        if core not in rl:
+            continue
+        role = rl.index(core)
+        got = len(chip_masks(topo, src, rl)[role])
+        rid, pid = topo.addr(dst, core)
+        m = topo.mask(core, dst)
+        for n in (("lu", "qp"), ("ll", "sp"))[role]:
+            b = T[n + "%d" % i]
+            ap = b[:].bitcast(dt.uint8) if n == "qp" else b[:]
+            g.wait_ge(T.sem[n + "%d" % i], got)
+            g.remote_dma(ap, ap, remote_sem=T.sem[n + "%d" % i], local_sem=T.sem.out, pid=pid, routing_id=rid,
+                         dma_engine_mask=m)
+            sent += len(topo.engines(core, dst))
+    if sent:
+        g.wait_ge(T.sem.out, sent)
+
+
+def tracker(g, T):
+    queues = {"ve": g.vector, "ac": g.scalar, "pe": g.tensor, "gp": g, "sy": g.sync}
+    clock = {q: {} for q in queues}
+    count = {q: 0 for q in queues}
+    snap, acc = {}, {}
+
+    def sync(q, reads, writes):
+        req = {}
+        for rw, regs in (("r", reads), ("w", writes)):
+            for buf, a, b, lane in regs:
+                for rw2, a2, b2, lane2, prod, cnt in acc.get(buf, []):
+                    if a2 >= b or a >= b2 or (lane is not None and lane2 is not None and lane != lane2):
+                        continue
+                    if rw == "r" and rw2 == "r" and (buf != "ps" or prod == q):
+                        continue
+                    req[prod] = max(req.get(prod, 0), cnt)
+        for p, n in req.items():
+            if clock[q].get(p, 0) >= n:
+                continue
+            if any(p2 != p and snap[(p2, n2)].get(p, 0) >= n for p2, n2 in req.items()):
+                continue
+            queues[q].wait_ge(T.sem[p], n)
+            for k, x in snap[(p, n)].items():
+                clock[q][k] = max(clock[q].get(k, 0), x)
+
+        for p, n in req.items():
+            clock[q][p] = max(clock[q].get(p, 0), n)
+
+    def note(prod, cnt, reads, writes):
+        for rw, regs in (("r", reads), ("w", writes)):
+            for buf, a, b, lane in regs:
+                old = acc.get(buf, [])
+                if rw == "w":
+                    old = [o for o in old if not (a <= o[1] and o[2] <= b and (lane is None or lane == o[3]))]
+                else:
+                    old = [o for o in old if not (o[0] == "r" and o[4] == prod and a <= o[1] and o[2] <= b
+                                                  and (lane is None or lane == o[3]))]
+                acc[buf] = old + [(rw, a, b, lane, prod, cnt)]
+
+    def op(q, fn, reads, writes):
+        sync(q, reads, writes)
+        count[q] += 1
+        fn(queues[q]).then_inc(T.sem[q], 1)
+        s = dict(clock[q])
+        s[q] = count[q]
+        snap[(q, count[q])] = s
+        note(q, count[q], reads, writes)
+
+    def dma(q, out, in_, reads, writes, sem):
+        sync(q, reads, writes)
+        queues[q].dma_start(out, in_).then_inc(T.sem[sem], 16)
+        s = dict(clock[q])
+        s[sem] = 16
+        snap[(sem, 16)] = s
+        note(sem, 16, reads, writes)
+
+    def arrive(sem, n, writes):
+        snap[(sem, n)] = {sem: n}
+        note(sem, n, [], writes)
+
+    return op, dma, arrive, sync, count
+
+
+def reg(buf, a=None, b=None, lane=None):
+    return (buf, 0 if a is None else a, 1 << 20 if b is None else b, lane)
+
+
+def rank_program(g, core, T, topo):
+    rank = T.rank_of(core)
+    if rank is None:
+        relay_program(g, core, T, topo)
+        return
+    op, dma, arrive, sync, count = tracker(g, T)
+    A = AluOpType
+    copy = ActivationFunctionType.Copy
+    outs = [0]
+
+    def fill(view, value, w):
+        op("ve", lambda e: e.memset(view, value), [], [w])
+
+    def iota(view, pattern, base, cm, w, small=False):
+        if small:
+            op("gp", lambda e: e.iota(view, pattern, base, cm, allow_small_or_imprecise_dtypes=True), [], [w])
+        else:
+            op("gp", lambda e: e.iota(view, pattern, base, cm), [], [w])
+
+    def ts(out, in0, s1, s2, op0, op1, r, w):
+        if op1 is None:
+            op("ve", lambda e: e.tensor_scalar(out, in0, s1, None, op0), r, w)
+        else:
+            op("ve", lambda e: e.tensor_scalar(out, in0, s1, s2, op0, op1), r, w)
+
+    def tt(out, in0, in1, o, r, w):
+        op("ve", lambda e: e.tensor_tensor(out, in0, in1, o), r, w)
+
+    def act(out, in_, r, w, scale=None):
+        if scale is None:
+            op("ac", lambda e: e.activation(out, in_, copy), r, w)
+        else:
+            op("ac", lambda e: e.activation(out, in_, copy, scale=scale), r, w)
+
+    def quant(qn, sn, a, b, tile, ta, tb):
+        op("ve", lambda e: e.quantize_mx(T[qn][:, a:b], T[sn][:, a:b], T[tile][:, 4 * ta:4 * tb]),
+           [reg(tile, ta, tb)], [reg(qn, a, b), reg(sn, a, b)])
+
+    def mul(bank, st, s0, mv, m0, m1):
+        qs, ss = "q" + st, "s" + st
+        qm, sm = "q" + mv, "s" + mv
+        n = m1 - m0
+        op("pe", lambda e: e.matmul_mx(T.ps[:, 512 * bank:512 * bank + n], T[qs][:, s0:s0 + 128], T[ss][:, s0:s0 + 128],
+                                       T[qm][:, m0:m1], T[sm][:, m0:m1], True, True),
+           [reg(qs, s0, s0 + 128), reg(ss, s0, s0 + 128), reg(qm, m0, m1), reg(sm, m0, m1)],
+           [reg("ps", 512 * bank, 512 * bank + 512)])
+
+    def bank(k):
+        return reg("ps", 512 * k, 512 * k + 512)
+
+    def pv(k):
+        return T.ps[:, 512 * k:512 * k + H]
+
+    dma("sy", T.x0[:, 0:576], T.x[:, 0:576], [], [reg("x0", 0, H)], "ldxu")
+    dma("ac", T.ut[:], T.u[:], [], [reg("ut")], "ldu")
+    dma("sy", T.x0[:, 576:1152], T.x[:, 576:1152], [], [reg("x0", H, C)], "ldxl")
+    dma("ac", T.mli[:], T.ml[:], [], [reg("mli")], "ldm")
+    dma("sy", T.qw[:].bitcast(dt.uint8), T.wc[:], [], [reg("qw")], "ldw")
+    dma("ac", T.sw[:], T.ws[:], [], [reg("sw")], "lds")
+    dma("sy", T.vt[:], T.v[:], [], [reg("vt")], "ldv")
+
+    iota(T.ul[:], [[16, 8]], 0, 0, reg("ul"))
+    iota(T.iom[:], [[1, 448]], 128, -1, reg("iom"))
+    iota(T.pc[:], [[0, 9]], 0, 1, reg("pc"))
+    iota(T.k16[:], [[16, 9]], 0, 0, reg("k16"))
+    iota(T.h[:], [[1, C]], -MID, 0, reg("h"), True)
+    iota(T.up[:, H:C], [[1, H]], C - MID, 0, reg("up", H, C), True)
+    fill(T.ones[:], 1.0, reg("ones"))
+    fill(T.rst[:], 1.0, reg("rst"))
+    fill(T.rst[:, 0:448:16], 0.0, reg("rst"))
+    fill(T.fl[:], 0.0, reg("fl"))
+    fill(T.mg[:, H:H + 16], 0.0, reg("mg", H, H + 16))
+    fill(T.lm[:], MID, reg("lm"))
+    fill(T.mm[:], 0.0, reg("mm"))
+    fill(T.nn[:], float(-MID), reg("nn"))
+    op("ve", lambda e: e.tensor_copy(T.uo[:], T.ul[:]), [reg("ul")], [reg("uo")])
+    ts(T.ioa[:], T.iom[:], 15, None, A.bitwise_and, None, [reg("iom")], [reg("ioa")])
+    ts(T.mskt[:, 0:304], T.ioa[:, 0:304], 0.0, float(H), A.is_equal, A.mult, [reg("ioa", 0, 304)], [reg("mskt", 0, 304)])
+    ts(T.mskt[:, 304:448], T.ioa[:, 304:448], 0.0, None, A.is_equal, None, [reg("ioa", 304, 448)], [reg("mskt", 304, 448)])
+    ts(T.pd[:], T.pc[:], 15, None, A.bitwise_and, None, [reg("pc")], [reg("pd")])
+    tt(T.idl[:], T.pd[:], T.k16[:], A.add, [reg("pd"), reg("k16")], [reg("idl")])
+    op("ve", lambda e: e.tensor_copy(T.lm[:, 19:28], T.idl[:]), [reg("idl")], [reg("lm", 19, 28)])
+    op("gp", lambda e: e.affine_select(T.idn[:], T.ones[:], [[-1, 128]], A.is_equal, 0.0, 0, 1), [reg("ones")], [reg("idn")])
+    iota(T.gtb[:, 0:H], [[1, H]], 0, 0, reg("gtb", 0, H), True)
+    iota(T.gtb[:, H:AW], [[1, C]], 0, 0, reg("gtb", H, AW), True)
+
+    op("ve", lambda e: e.quantize_mx(T.qu[:], T.su[:], T.ut[:]), [reg("ut")], [reg("qu"), reg("su")])
+    op("ve", lambda e: e.tensor_copy(T.qr[:, 0:128].bitcast(dt.uint32), T.qu[:, 0:128].bitcast(dt.uint32).indirect(T.uo[:, 0:8])),
+       [reg("qu"), reg("uo")], [reg("qr")])
+    op("ve", lambda e: e.tensor_copy(T.sr[:, 0:128], T.su[:, 0:128].indirect(T.uo[:, 0:8])), [reg("su"), reg("uo")], [reg("sr")])
+
+    def state_half(k, lo):
+        a = H if lo else 0
+
+        def planes():
+            for b in range(4):
+                act(T.xp[:, C * b + a:C * b + a + H], T["x%d" % k][:, 4 * a + b:4 * (a + H):4], [reg("x%d" % k, a, a + H, b)],
+                    [reg("xp", C * b + a, C * b + a + H)])
+        if 0 < k < ROUNDS:
+            planes()
+        quant("qx", "sx", a, a + H, "x%d" % k, a, a + H)
+        if k < ROUNDS:
+            mul(4 + lo, "r", 0, "x", a, a + H)
+            if not lo:
+                act(T.scu[:], pv(4), [bank(4)], [reg("scu")])
+            if k == 0:
+                planes()
+        else:
+            dma("sy", T.oc[:, 4 * a:4 * a + 4 * H], T.qx[:, a:a + H].bitcast(dt.uint8), [reg("qx", a, a + H)], [], "stc%d" % lo)
+            mul(4 + lo, "v", 0, "x", a, a + H)
+            act(T.ys[:, a:a + H], pv(4 + lo), [bank(4 + lo)], [reg("ys", a, a + H)])
+            dma("ac", T.y[:, a:a + H], T.ys[:, a:a + H], [reg("ys", a, a + H)], [], "sty%d" % lo)
+
+    op("ve", lambda e: e.tensor_copy(T.mlf[:, 0:18], T.mli[:]), [reg("mli")], [reg("mlf")])
+    ts(T.mlg[:, 0:18], T.mlf[:, 0:18], float(H), float(H), A.is_ge, A.mult, [reg("mlf")], [reg("mlg")])
+    tt(T.mlh[:, 0:18], T.mlf[:, 0:18], T.mlg[:, 0:18], A.add, [reg("mlf"), reg("mlg")], [reg("mlh")])
+    for a, b in ((0, 0), (10, 9)):
+        op("ve", lambda e: e.tensor_copy(T.lm[:, a:a + 9], T.mlh[:, b:b + 9]), [reg("mlh")], [reg("lm", a, a + 9)])
+    tt(T.mli2[:, 0:18], T.mlf[:, 0:18], T.mlg[:, 0:18], A.subtract, [reg("mlf"), reg("mlg")], [reg("mli2")])
+    for a, b in ((0, 0), (10, 9)):
+        ts(T.mm[:, a:a + 9], T.mli2[:, b:b + 9], float(-MID), None, A.add, None, [reg("mli2")], [reg("mm", a, a + 9)])
+    state_half(0, 0)
+    state_half(0, 1)
+    for t in ("ta", "tb", "tc"):
+        act(T[t][:, 0:H], T.h[:, 0:H], [reg("h", 0, H)], [reg(t, 0, H)])
+        act(T[t][:, C:AW], T.up[:, H:C], [reg("up", H, C)], [reg(t, C, AW)])
+    act(T.vtab[:, H:C], T.up[:, H:C], [reg("up", H, C)], [reg("vtab", H, C)])
+
+    def spread(n0, n1, last):
+        op("ve", lambda e: e.tensor_tensor_scan(T.sc[:, n0:n1], T.rst[:, n0:n1], T.mg[:, n0:n1], 0.0, A.mult, A.add),
+           [reg("rst"), reg("mg", n0, n1)], [reg("sc", n0, n1)])
+        buf, w = last
+        ts(T[buf][:, 0:w], T.sc[:, n0 + 15:n1:16], float(MID), None, A.add, None, [reg("sc", n0, n1)], [reg(buf, 0, w)])
+
+    def gather(q, out, win, width, off, o0, o1, w, mask=None):
+        src = T[win][:, 0:width].indirect(T[off][:, o0:o1])
+        r = [reg(win, 0, width), reg(off, o0, o1)]
+        if mask is not None:
+            tt(out, src, T.msk[:, mask:mask + 16 * (o1 - o0)], A.mult, r + [reg("msk")], [w])
+        elif q == "ve":
+            op("ve", lambda e: e.tensor_copy(out, src), r, [w])
+        else:
+            act(out, src, r, [w])
+
+    for i, s in enumerate(STEP):
+        x, xn, na, lu, ll = "x%d" % i, "x%d" % (i + 1), "na%d" % i, "lu%d" % i, "ll%d" % i
+        qa, qp = "a%d" % i, "p%d" % i
+        dst = T.cores[rank ^ s]
+        rl = relays(topo, core, dst)
+        em = chip_masks(topo, core, rl)
+        ids = []
+        for k in rl:
+            rid, pid = topo.addr(k, core)
+            ids.append((rid, pid))
+        back = relays(topo, dst, core)
+        n_in = [len(topo.engines(k, core)) for k in back]
+        arrive(lu, n_in[0], [reg(lu)])
+        arrive("q" + qp, n_in[0], [reg("q" + qp)])
+        arrive(ll, n_in[1], [reg(ll)])
+        arrive("s" + qp, n_in[1], [reg("s" + qp)])
+
+        tt(T.fl[:, 0:H], T.scu[:], pv(5), A.is_gt, [reg("scu"), bank(5)], [reg("fl", 0, H)])
+        tt(T.fl[:, C:AW], T.scu[:], pv(5), A.is_le, [reg("scu"), bank(5)], [reg("fl", C, AW)])
+        tt(T.mgt[:], T.fl[:, 0:AW].indirect(T.lm[:, 0:28]), T.mskt[:], A.mult, [reg("fl"), reg("lm"), reg("mskt")], [reg("mgt")])
+        op("ve", lambda e: e.tensor_tensor_scan(T.sct[:], T.rst[:], T.mgt[:], 0.0, A.mult, A.add),
+           [reg("rst"), reg("mgt")], [reg("sct")])
+        tt(T.w1[:, 0:19], T.mm[:, 0:19], T.sct[:, 15:304:16], A.add, [reg("mm"), reg("sct")], [reg("w1")])
+        tt(T.d1[:, 0:9], T.w1[:, 10:19], T.w1[:, 0:9], A.subtract, [reg("w1")], [reg("d1")])
+        tt(T.e1[:, 0:9], T.d1[:, 0:9], T.sct[:, 319:448:16], A.mult, [reg("d1"), reg("sct")], [reg("e1")])
+        tt(T.nn[:, 0:9], T.w1[:, 0:9], T.e1[:, 0:9], A.add, [reg("w1"), reg("e1")], [reg("nn", 0, 9)])
+        tt(T.nn[:, 10:19], T.w1[:, 10:19], T.e1[:, 0:9], A.subtract, [reg("w1"), reg("e1")], [reg("nn", 10, 19)])
+        ts(T[na][:], T.nn[:], float(MID), None, A.add, None, [reg("nn")], [reg(na)])
+        sync("gp", [reg(na)], [])
+        g.remote_dma_fused([
+            RemoteDMATransfer(dst_ids=[DstId(rid=ids[0][0], pnc=ids[0][1])], dma_engine_mask=bits(em[0]),
+                              remote_sem=T.sem[lu], src=T[na][:, 0:10], dst=T[lu][:]),
+            RemoteDMATransfer(dst_ids=[DstId(rid=ids[1][0], pnc=ids[1][1])], dma_engine_mask=bits(em[1]),
+                              remote_sem=T.sem[ll], src=T[na][:, 10:20], dst=T[ll][:])], local_sem=T.sem.out)
+        outs[0] += len(em[0]) + len(em[1])
+        gather("ac", T.up[:, 0:H], "h", C, na, 10, 19, reg("up", 0, H))
+
+        def z_half(lo):
+            a, o = (H, 10) if lo else (0, 0)
+            for b in range(4):
+                tt(T.z[:, 4 * a + b:4 * (a + H):4], T.xp[:, C * b:C * b + C].indirect(T[na][:, o:o + 9]),
+                   T[x][:, 4 * a + b:4 * (a + H):4], A.add, [reg(x, a, a + H, b), reg("xp", C * b, C * b + C), reg(na, o, o + 9)],
+                   [reg("z", a, a + H, b)])
+            quant("qz", "sz", a, a + H, "z", a, a + H)
+
+        def a_half(lo):
+            a, k = (H, 0) if lo else (0, 4)
+            for b in range(4):
+                mul(k + b, "w", 128 * b, "z", a, a + H)
+            for b in range(4):
+                act(T.a[:, 4 * a + b:4 * (a + H):4], pv(k + b), [bank(k + b)], [reg("a", a, a + H, b)], scale=0.015625)
+
+        z_half(1)
+        a_half(1)
+        z_half(0)
+        a_half(0)
+        quant("q" + qa, "s" + qa, H, C, "a", H, C)
+        for n, k, view in (("q", 0, T["q" + qa][:, H:C].bitcast(dt.uint8)), ("s", 1, T["s" + qa][:, H:C])):
+            sync("gp", [reg(n + qa, H, C)], [])
+            land = T[n + qp][:].bitcast(dt.uint8) if n == "q" else T[n + qp][:]
+            g.remote_dma(land, view, remote_sem=T.sem[n + qp], local_sem=T.sem.out, pid=ids[k][1], routing_id=ids[k][0],
+                         dma_engine_mask=bits(em[k]))
+            outs[0] += len(em[k])
+        if i == 0:
+            ts(T.msk[:], T.ioa[:, 0:304], 0.0, None, A.is_equal, None, [reg("ioa", 0, 304)], [reg("msk")])
+            fill(T.et[:], 0.0, reg("et"))
+            for b in range(4):
+                op("ve", lambda e: e.tensor_copy(T.et[:, 513 * b:512 * b + 512:4], T.idn[:]), [reg("idn"), reg("et", 128 * b, 128 * b + 128)],
+                   [reg("et", 128 * b, 128 * b + 128, b)])
+            op("ve", lambda e: e.quantize_mx(T.qe[:], T.se[:], T.et[:]), [reg("et")], [reg("qe"), reg("se")])
+        quant("q" + qa, "s" + qa, 0, H, "a", 0, H)
+        if i == 0:
+            op("ve", lambda e: e.quantize_mx(T.qv[:], T.sv[:], T.vt[:]), [reg("vt")], [reg("qv"), reg("sv")])
+            for b in range(4):
+                fill(T.db[:, AW * b + H:AW * b + C], 0.0, reg("db", AW * b + H, AW * b + C))
+        for b in range(4):
+            mul(b, "e", 128 * b, qa, 0, H)
+        for b in range(4):
+            act(T.db[:, AW * b:AW * b + H], pv(b), [bank(b)], [reg("db", AW * b, AW * b + H)])
+        for b in range(4):
+            mul(4 + b, "e", 128 * b, qp, 0, H)
+
+        def table(t):
+            return T[t][:, H:C], reg(t, H, C)
+        mgu, mgl = (T.mg[:, 0:H], reg("mg", 0, H)), (T.mg[:, 160:304], reg("mg", 160, 304))
+        gather("ve", mgu[0], "up", C, lu, 0, 9, mgu[1], 0)
+        v, w = table("ta")
+        gather("ac", v, "up", C, lu, 0, 9, w)
+        spread(0, H, ("lk0", 9))
+        v, w = table("tb")
+        gather("ve", v, "ta", AW, "lk0", 0, 9, w)
+        now, lk = "tb", 0
+        for t in ("tc", "ta", "tb", "tc"):
+            gather("ve", mgu[0], now, AW, "lk%d" % lk, 0, 9, mgu[1], 0)
+            v, w = table(t)
+            gather("ac", v, now, AW, "lk%d" % lk, 0, 9, w)
+            lk = 1 - lk
+            spread(0, H, ("lk%d" % lk, 9))
+            now = t
+        for t in ("ta", "tb"):
+            v, w = table(t)
+            gather("ve", v, now, AW, "lk%d" % lk, 0, 9, w)
+            now = t
+        gather("ac", T.vtab[:, 0:H], now, AW, na, 10, 19, reg("vtab", 0, H))
+        gather("ve", mgu[0], now, AW, na, 0, 9, mgu[1], 0)
+        gather("ve", mgl[0], "vtab", C, ll, 0, 9, mgl[1], 160)
+        spread(0, 304, ("lm", 19))
+        for b in range(4):
+            act(T.db[:, AW * b + C:AW * b + AW], pv(4 + b), [bank(4 + b)], [reg("db", AW * b + C, AW * b + AW)])
+        if i + 1 == ROUNDS:
+            gather("ac", T.mrow[:], "gtb", AW, "lm", 0, 19, reg("mrow"))
+            dma("sy", T.mo[:, 0:H], T.mrow[0:128:16, 0:H], [reg("mrow")], [], "stm0")
+            dma("sy", T.mo[:, H:C], T.mrow[0:128:16, 160:304], [reg("mrow")], [], "stm1")
+        for lo in (0, 1):
+            a, o = (H, 10) if lo else (0, 0)
+            for b in range(4):
+                tt(T[xn][:, 4 * a + b:4 * (a + H):4], T.db[:, AW * b:AW * b + AW].indirect(T.lm[:, o:o + 9]),
+                   T[x][:, 4 * a + b:4 * (a + H):4], A.add, [reg("db", AW * b, AW * b + AW), reg("lm", o, o + 9), reg(x, a, a + H, b)],
+                   [reg(xn, a, a + H, b)])
+            state_half(i + 1, lo)
+        if i + 1 < ROUNDS:
+            sv = T.sc[:, 15:304:16]
+            ts(T.mt[:, 0:19], sv, 0.0, float(-C), A.is_ge, A.mult, [reg("sc")], [reg("mt")])
+            tt(T.mm[:, 0:19], T.mt[:, 0:19], sv, A.add, [reg("mt"), reg("sc")], [reg("mm")])
+    for k in range(4):
+        dma("sy" if k % 2 else "ac", T.osc[4 * k:4 * k + 4, :], T.sx[32 * k:32 * k + 4, :], [reg("sx")], [], "sts%d" % k)
+    for n in ("ve", "ac", "pe", "gp"):
+        g.wait_ge(T.sem[n], count[n])
+    for n in LOADS + STORES:
+        g.wait_ge(T.sem[n], 16)
+    g.wait_ge(T.sem.out, outs[0])

@@ -3,11 +3,14 @@ from concourse.mybir import dt, AluOpType, ActivationFunctionType
 
 C, H = 288, 144
 STEP = (4, 1, 2)
-AW, MID = 432, 216
+AW, MID = 576, 144
+BIG = 576
+LOW = MID + BIG
+OFF, TW = 100, 188
 ROUNDS = len(STEP)
 
 SCRATCH = {}
-for _n in ("x0", "x1", "x2", "x3", "z", "a"):
+for _n in ("x0", "x1", "x2", "x3", "z", "a", "xp", "db"):
     SCRATCH[_n] = ("sbuf", [128, 4 * C], "bfloat16")
 for _n in ["x", "z"] + ["a%d" % i for i in range(ROUNDS)]:
     SCRATCH["q" + _n] = ("sbuf", [128, C], "float8_e4m3fn_x4")
@@ -15,8 +18,7 @@ for _n in ["x", "z"] + ["a%d" % i for i in range(ROUNDS)]:
 for _n in range(ROUNDS):
     SCRATCH["qp%d" % _n] = ("sbuf", [128, H], "float8_e4m3fn_x4")
     SCRATCH["sp%d" % _n] = ("sbuf", [128, H], "uint8")
-    SCRATCH["lu%d" % _n] = ("sbuf", [128, 10], "uint16")
-    SCRATCH["ll%d" % _n] = ("sbuf", [128, 10], "uint16")
+    SCRATCH["lp%d" % _n] = ("sbuf", [128, 20], "uint16")
     SCRATCH["na%d" % _n] = ("sbuf", [128, 20], "uint16")
 for _n in ("u", "v"):
     SCRATCH[_n + "t"] = ("sbuf", [128, 512], "bfloat16")
@@ -26,74 +28,71 @@ for _n in ("u", "r", "v"):
 for _n in ("w", "e"):
     SCRATCH["q" + _n] = ("sbuf", [128, 512], "float8_e4m3fn_x4")
     SCRATCH["s" + _n] = ("sbuf", [128, 512], "uint8")
+for _n in ("idt", "ta", "tb", "tc", "zg", "dg"):
+    SCRATCH[_n] = ("sbuf", [128, AW], "bfloat16")
+for _n in ("up", "vtab", "fl", "fr"):
+    SCRATCH[_n] = ("sbuf", [128, C], "bfloat16")
+for _n in ("sv0", "mt", "mu", "d1", "e1", "nn"):
+    SCRATCH[_n] = ("sbuf", [128, 20], "float32")
 SCRATCH.update({
     "et": ("sbuf", [128, 2048], "bfloat16"),
     "ones": ("sbuf", [128, 128], "bfloat16"),
     "idn": ("sbuf", [128, 128], "bfloat16"),
     "mli": ("sbuf", [128, 18], "int32"),
-    "mlf": ("sbuf", [128, 20], "float32"),
-    "mlg": ("sbuf", [128, 20], "float32"),
-    "mlh": ("sbuf", [128, 20], "float32"),
-    "mli2": ("sbuf", [128, 20], "float32"),
-    "lm": ("sbuf", [128, 28], "uint16"),
-    "mm": ("sbuf", [128, 20], "float32"),
-    "mt": ("sbuf", [128, 20], "float32"),
-    "w1": ("sbuf", [128, 20], "float32"),
-    "d1": ("sbuf", [128, 10], "float32"),
-    "e1": ("sbuf", [128, 10], "float32"),
-    "nn": ("sbuf", [128, 20], "float32"),
-    "xp": ("sbuf", [128, 4 * C], "bfloat16"),
-    "fl": ("sbuf", [128, AW], "bfloat16"),
-    "scu": ("sbuf", [128, H], "float32"),
-    "mgt": ("sbuf", [128, 448], "bfloat16"),
-    "sct": ("sbuf", [128, 448], "bfloat16"),
-    "mskt": ("sbuf", [128, 448], "bfloat16"),
-    "rst": ("sbuf", [128, 448], "bfloat16"),
-    "msk": ("sbuf", [128, 304], "bfloat16"),
-    "mg": ("sbuf", [128, 304], "bfloat16"),
-    "sc": ("sbuf", [128, 304], "bfloat16"),
-    "h": ("sbuf", [128, C], "bfloat16"),
-    "up": ("sbuf", [128, C], "bfloat16"),
-    "vtab": ("sbuf", [128, C], "bfloat16"),
-    "ta": ("sbuf", [128, AW], "bfloat16"),
-    "tb": ("sbuf", [128, AW], "bfloat16"),
-    "tc": ("sbuf", [128, AW], "bfloat16"),
-    "gtb": ("sbuf", [128, AW], "float32"),
+    "lm": ("sbuf", [128, 20], "uint16"),
+    "scl": ("sbuf", [128, H], "float32"),
+    "gt": ("sbuf", [128, 304], "bfloat16"),
+    "sct": ("sbuf", [128, 304], "bfloat16"),
+    "scf": ("sbuf", [128, H], "bfloat16"),
+    "ct": ("sbuf", [128, 304], "bfloat16"),
+    "cf": ("sbuf", [128, H], "bfloat16"),
+    "cg": ("sbuf", [128, H], "bfloat16"),
+    "sc": ("sbuf", [128, H], "float16"),
+    "scg": ("sbuf", [128, 304], "float16"),
     "lk0": ("sbuf", [128, 10], "uint16"),
     "lk1": ("sbuf", [128, 10], "uint16"),
-    "db": ("sbuf", [128, 4 * AW], "bfloat16"),
-    "mrow": ("sbuf", [128, 304], "float32"),
+    "mrow": ("sbuf", [128, C], "float32"),
     "ys": ("sbuf", [128, C], "float32"),
-    "iom": ("sbuf", [128, 448], "int32"),
-    "ioa": ("sbuf", [128, 448], "int32"),
     "ul": ("sbuf", [128, 8], "int32"),
     "uo": ("sbuf", [128, 8], "uint16"),
-    "pc": ("sbuf", [128, 9], "int32"),
-    "pd": ("sbuf", [128, 9], "int32"),
-    "k16": ("sbuf", [128, 9], "int32"),
-    "idl": ("sbuf", [128, 9], "int32"),
+    "pc": ("sbuf", [128, 20], "int32"),
+    "pd": ("sbuf", [128, 20], "int32"),
+    "pl": ("sbuf", [128, 20], "uint16"),
+    "pm": ("sbuf", [128, 1], "float32"),
+    "c0": ("sbuf", [128, 1], "float32"),
+    "col": ("sbuf", [128, 48], "float32"),
+    "eq": ("sbuf", [128, 48], "float32"),
+    "lt": ("sbuf", [128, 48], "float32"),
+    "pat": ("sbuf", [128, 48], "bfloat16"),
     "ps": ("psum", [128, 4096], "float32"),
 })
 LOADS = ["ldxu", "ldxl", "ldu", "ldm", "ldw", "lds", "ldv"]
-STORES = ["sty0", "sty1", "stc0", "stc1", "sts0", "sts1", "sts2", "sts3", "stm0", "stm1"]
+STORES = ["sty0", "sty1", "stc0", "stc1", "sts0", "sts1", "sts2", "sts3", "stm"]
 SEMAPHORES = (["ve", "ac", "pe", "gp", "out"] + LOADS + STORES
-              + [n + "%d" % i for n in ("lu", "ll", "qp", "sp") for i in range(ROUNDS)])
+              + [n + "%d" % i for n in ("lp", "qp", "sp") for i in range(ROUNDS)])
 
 
 def relays(topo, src, dst):
     ks = [k for k in topo.cores_of(src) if k != src and topo.may_write(k, dst)]
-    return sorted(ks, key=lambda k: (topo.die(k) != topo.die(src), k))[:2]
+    near = [k for k in ks if topo.die(k) == topo.die(src)]
+    far = [k for k in ks if topo.die(k) != topo.die(src)]
+    return [near[0], near[1], far[0]]
 
 
 def bits(es):
     return sum(1 << e for e in es)
 
 
-def chip_masks(topo, src, rl):
-    e = topo.engines(src, rl[0])
-    f = topo.engines(src, rl[1])
+def halves(topo, src, rl):
+    e = topo.engines(src, rl[1])
+    f = topo.engines(src, rl[2])
     n = len(e) // 2
     return [e[:n], [k for k in f if k not in e[:n]][:n]]
+
+
+def code_half(T, name, first, k):
+    a = first + k * H // 2
+    return T[name][:, a:a + H // 2].bitcast(dt.uint8)
 
 
 def relay_program(g, core, T, topo):
@@ -109,15 +108,15 @@ def relay_program(g, core, T, topo):
         if core not in rl:
             continue
         role = rl.index(core)
-        got = len(chip_masks(topo, src, rl)[role])
         rid, pid = topo.addr(dst, core)
-        m = topo.mask(core, dst)
-        for n in (("lu", "qp"), ("ll", "sp"))[role]:
-            b = T[n + "%d" % i]
-            ap = b[:].bitcast(dt.uint8) if n == "qp" else b[:]
-            g.wait_ge(T.sem[n + "%d" % i], got)
-            g.remote_dma(ap, ap, remote_sem=T.sem[n + "%d" % i], local_sem=T.sem.out, pid=pid, routing_id=rid,
-                         dma_engine_mask=m)
+        if role == 0:
+            jobs = [(n + "%d" % i, T[n + "%d" % i][:], len(topo.engines(src, core))) for n in ("lp", "sp")]
+        else:
+            jobs = [("qp%d" % i, code_half(T, "qp%d" % i, 0, role - 1), len(halves(topo, src, rl)[role - 1]))]
+        for sem, ap, got in jobs:
+            g.wait_ge(T.sem[sem], got)
+            g.remote_dma(ap, ap, remote_sem=T.sem[sem], local_sem=T.sem.out, pid=pid, routing_id=rid,
+                         dma_engine_mask=topo.mask(core, dst))
             sent += len(topo.engines(core, dst))
     if sent:
         g.wait_ge(T.sem.out, sent)
@@ -224,6 +223,14 @@ def rank_program(g, core, T, topo):
         else:
             op("ac", lambda e: e.activation(out, in_, copy, scale=scale), r, w)
 
+    def cp(q, out, in_, r, w, scale=None):
+        if q == "ac":
+            act(out, in_, r, w, scale)
+        elif scale is None:
+            op("ve", lambda e: e.tensor_copy(out, in_), r, w)
+        else:
+            ts(out, in_, scale, None, A.mult, None, r, w)
+
     def quant(qn, sn, a, b, tile, ta, tb):
         op("ve", lambda e: e.quantize_mx(T[qn][:, a:b], T[sn][:, a:b], T[tile][:, 4 * ta:4 * tb]),
            [reg(tile, ta, tb)], [reg(qn, a, b), reg(sn, a, b)])
@@ -243,223 +250,230 @@ def rank_program(g, core, T, topo):
     def pv(k):
         return T.ps[:, 512 * k:512 * k + H]
 
-    dma("sy", T.x0[:, 0:576], T.x[:, 0:576], [], [reg("x0", 0, H)], "ldxu")
+    def gather(q, out, w, win, a, b, off, o, n=9, scale=None):
+        cp(q, out, T[win][:, a:b].indirect(T[off][:, o:o + n]), [reg(win, a, b), reg(off, o, o + n)], [w], scale)
+
+    def pick(out, w, data, r, const, n, start):
+        op("ve", lambda e: e.tensor_tensor_scan(out, data, T[const][:, 0:n], start, A.max, A.add), [r, reg(const)], [w])
+
+    def nodes(t):
+        return T[t][:, 1:C:2], reg(t, 0, C, 1)
+
     dma("ac", T.ut[:], T.u[:], [], [reg("ut")], "ldu")
     dma("sy", T.x0[:, 576:1152], T.x[:, 576:1152], [], [reg("x0", H, C)], "ldxl")
+    dma("sy", T.x0[:, 0:576], T.x[:, 0:576], [], [reg("x0", 0, H)], "ldxu")
     dma("ac", T.mli[:], T.ml[:], [], [reg("mli")], "ldm")
     dma("sy", T.qw[:].bitcast(dt.uint8), T.wc[:], [], [reg("qw")], "ldw")
-    dma("ac", T.sw[:], T.ws[:], [], [reg("sw")], "lds")
+    dma("sy", T.sw[:], T.ws[:], [], [reg("sw")], "lds")
     dma("sy", T.vt[:], T.v[:], [], [reg("vt")], "ldv")
 
+    iota(T.pc[:], [[0, 20]], 0, 1, reg("pc"))
+    iota(T.col[:], [[0, 3], [1, 16]], 0, 0, reg("col"), True)
     iota(T.ul[:], [[16, 8]], 0, 0, reg("ul"))
-    iota(T.iom[:], [[1, 448]], 128, -1, reg("iom"))
-    iota(T.pc[:], [[0, 9]], 0, 1, reg("pc"))
-    iota(T.k16[:], [[16, 9]], 0, 0, reg("k16"))
-    iota(T.h[:], [[1, C]], -MID, 0, reg("h"), True)
-    iota(T.up[:, H:C], [[1, H]], C - MID, 0, reg("up", H, C), True)
+    iota(T.idt[:], [[1, AW]], -MID, 0, reg("idt"), True)
     fill(T.ones[:], 1.0, reg("ones"))
-    fill(T.rst[:], 1.0, reg("rst"))
-    fill(T.rst[:, 0:448:16], 0.0, reg("rst"))
-    fill(T.fl[:], 0.0, reg("fl"))
-    fill(T.mg[:, H:H + 16], 0.0, reg("mg", H, H + 16))
-    fill(T.lm[:], MID, reg("lm"))
-    fill(T.mm[:], 0.0, reg("mm"))
-    fill(T.nn[:], float(-MID), reg("nn"))
-    op("ve", lambda e: e.tensor_copy(T.uo[:], T.ul[:]), [reg("ul")], [reg("uo")])
-    ts(T.ioa[:], T.iom[:], 15, None, A.bitwise_and, None, [reg("iom")], [reg("ioa")])
-    ts(T.mskt[:, 0:304], T.ioa[:, 0:304], 0.0, float(H), A.is_equal, A.mult, [reg("ioa", 0, 304)], [reg("mskt", 0, 304)])
-    ts(T.mskt[:, 304:448], T.ioa[:, 304:448], 0.0, None, A.is_equal, None, [reg("ioa", 304, 448)], [reg("mskt", 304, 448)])
+    fill(T.lm[:], 0, reg("lm"))
+    fill(T.nn[:], float(-TW), reg("nn"))
+    fill(T.sv0[:], float(-LOW), reg("sv0"))
     ts(T.pd[:], T.pc[:], 15, None, A.bitwise_and, None, [reg("pc")], [reg("pd")])
-    tt(T.idl[:], T.pd[:], T.k16[:], A.add, [reg("pd"), reg("k16")], [reg("idl")])
-    op("ve", lambda e: e.tensor_copy(T.lm[:, 19:28], T.idl[:]), [reg("idl")], [reg("lm", 19, 28)])
+    cp("ve", T.pm[:], T.pd[:, 0:1], [reg("pd")], [reg("pm")])
+    cp("ve", T.pl[:], T.pd[:], [reg("pd")], [reg("pl")])
+    ts(T.eq[:], T.col[:], T.pm[:], None, A.is_equal, None, [reg("col"), reg("pm")], [reg("eq")])
+    ts(T.lt[:], T.col[:], T.pm[:], None, A.is_lt, None, [reg("col"), reg("pm")], [reg("lt")])
+    cp("ve", T.uo[:], T.ul[:], [reg("ul")], [reg("uo")])
+    tt(T.pat[:], T.eq[:], T.lt[:], A.subtract, [reg("eq"), reg("lt")], [reg("pat")])
+    ts(T.c0[:], T.eq[:, 15:16], 2.0, float(LOW - 290), A.mult, A.add, [reg("eq")], [reg("c0")])
+    ts(T.pat[:, 31:32], T.eq[:, 15:16], -1.5, None, A.add, None, [reg("eq")], [reg("pat", 31, 32)])
+    ts(T.pat[:, 47:48], T.eq[:, 15:16], -2.0, None, A.add, None, [reg("eq")], [reg("pat", 47, 48)])
+    gather("ac", T.ct[:], reg("ct"), "pat", 0, 16, "pl", 0, 19, 2.0)
+    gather("ac", T.cf[:], reg("cf"), "pat", 16, 32, "pl", 0, 9, 2.0)
     op("gp", lambda e: e.affine_select(T.idn[:], T.ones[:], [[-1, 128]], A.is_equal, 0.0, 0, 1), [reg("ones")], [reg("idn")])
-    iota(T.gtb[:, 0:H], [[1, H]], 0, 0, reg("gtb", 0, H), True)
-    iota(T.gtb[:, H:AW], [[1, C]], 0, 0, reg("gtb", H, AW), True)
+    fill(T.et[:], 0.0, reg("et"))
 
     op("ve", lambda e: e.quantize_mx(T.qu[:], T.su[:], T.ut[:]), [reg("ut")], [reg("qu"), reg("su")])
     op("ve", lambda e: e.tensor_copy(T.qr[:, 0:128].bitcast(dt.uint32), T.qu[:, 0:128].bitcast(dt.uint32).indirect(T.uo[:, 0:8])),
        [reg("qu"), reg("uo")], [reg("qr")])
-    op("ve", lambda e: e.tensor_copy(T.sr[:, 0:128], T.su[:, 0:128].indirect(T.uo[:, 0:8])), [reg("su"), reg("uo")], [reg("sr")])
+    act(T.sr[:, 0:128], T.su[:, 0:128].indirect(T.uo[:, 0:8]), [reg("su"), reg("uo")], [reg("sr")])
+
+    def planes(k, lo):
+        for b in range(4):
+            act(T.xp[:, C * b + lo:C * b + C:2], T["x%d" % k][:, 4 * H * lo + b:4 * H * (lo + 1):4],
+                [reg("x%d" % k, H * lo, H * lo + H, b)], [reg("xp", C * b, C * b + C, lo)])
 
     def state_half(k, lo):
-        a = H if lo else 0
-
-        def planes():
-            for b in range(4):
-                act(T.xp[:, C * b + a:C * b + a + H], T["x%d" % k][:, 4 * a + b:4 * (a + H):4], [reg("x%d" % k, a, a + H, b)],
-                    [reg("xp", C * b + a, C * b + a + H)])
-        if 0 < k < ROUNDS:
-            planes()
+        a = H * lo
         quant("qx", "sx", a, a + H, "x%d" % k, a, a + H)
         if k < ROUNDS:
-            mul(4 + lo, "r", 0, "x", a, a + H)
-            if not lo:
-                act(T.scu[:], pv(4), [bank(4)], [reg("scu")])
-            if k == 0:
-                planes()
+            mul(lo, "r", 0, "x", a, a + H)
+            if lo:
+                act(T.scl[:], pv(1), [bank(1)], [reg("scl")])
+            planes(k, lo)
         else:
             dma("sy", T.oc[:, 4 * a:4 * a + 4 * H], T.qx[:, a:a + H].bitcast(dt.uint8), [reg("qx", a, a + H)], [], "stc%d" % lo)
-            mul(4 + lo, "v", 0, "x", a, a + H)
-            act(T.ys[:, a:a + H], pv(4 + lo), [bank(4 + lo)], [reg("ys", a, a + H)])
+            mul(lo, "v", 0, "x", a, a + H)
+            act(T.ys[:, a:a + H], pv(lo), [bank(lo)], [reg("ys", a, a + H)])
             dma("ac", T.y[:, a:a + H], T.ys[:, a:a + H], [reg("ys", a, a + H)], [], "sty%d" % lo)
 
-    op("ve", lambda e: e.tensor_copy(T.mlf[:, 0:18], T.mli[:]), [reg("mli")], [reg("mlf")])
-    ts(T.mlg[:, 0:18], T.mlf[:, 0:18], float(H), float(H), A.is_ge, A.mult, [reg("mlf")], [reg("mlg")])
-    tt(T.mlh[:, 0:18], T.mlf[:, 0:18], T.mlg[:, 0:18], A.add, [reg("mlf"), reg("mlg")], [reg("mlh")])
+    def mates_mod(sv, r):
+        ts(T.mt[:, 0:19], sv, float(C - LOW), float(-C), A.is_ge, A.mult, [r], [reg("mt")])
+        ts(T.mu[:, 0:19], sv, T.c0[:], None, A.add, None, [r, reg("c0")], [reg("mu")])
+        tt(T.ct[:, 15:304:16], T.mt[:, 0:19], T.mu[:, 0:19], A.add, [reg("mt"), reg("mu")], [reg("ct")])
+
     for a, b in ((0, 0), (10, 9)):
-        op("ve", lambda e: e.tensor_copy(T.lm[:, a:a + 9], T.mlh[:, b:b + 9]), [reg("mlh")], [reg("lm", a, a + 9)])
-    tt(T.mli2[:, 0:18], T.mlf[:, 0:18], T.mlg[:, 0:18], A.subtract, [reg("mlf"), reg("mlg")], [reg("mli2")])
-    for a, b in ((0, 0), (10, 9)):
-        ts(T.mm[:, a:a + 9], T.mli2[:, b:b + 9], float(-MID), None, A.add, None, [reg("mli2")], [reg("mm", a, a + 9)])
-    state_half(0, 0)
+        cp("ve", T.lm[:, a:a + 9], T.mli[:, b:b + 9], [reg("mli")], [reg("lm", a, a + 9)])
+        ts(T.sv0[:, a:a + 9], T.mli[:, b:b + 9], 2.0, float(-LOW), A.mult, A.add, [reg("mli")], [reg("sv0", a, a + 9)])
     state_half(0, 1)
-    for t in ("ta", "tb", "tc"):
-        act(T[t][:, 0:H], T.h[:, 0:H], [reg("h", 0, H)], [reg(t, 0, H)])
-        act(T[t][:, C:AW], T.up[:, H:C], [reg("up", H, C)], [reg(t, C, AW)])
-    act(T.vtab[:, H:C], T.up[:, H:C], [reg("up", H, C)], [reg("vtab", H, C)])
-
-    def spread(n0, n1, last):
-        op("ve", lambda e: e.tensor_tensor_scan(T.sc[:, n0:n1], T.rst[:, n0:n1], T.mg[:, n0:n1], 0.0, A.mult, A.add),
-           [reg("rst"), reg("mg", n0, n1)], [reg("sc", n0, n1)])
-        buf, w = last
-        ts(T[buf][:, 0:w], T.sc[:, n0 + 15:n1:16], float(MID), None, A.add, None, [reg("sc", n0, n1)], [reg(buf, 0, w)])
-
-    def gather(q, out, win, width, off, o0, o1, w, mask=None):
-        src = T[win][:, 0:width].indirect(T[off][:, o0:o1])
-        r = [reg(win, 0, width), reg(off, o0, o1)]
-        if mask is not None:
-            tt(out, src, T.msk[:, mask:mask + 16 * (o1 - o0)], A.mult, r + [reg("msk")], [w])
-        elif q == "ve":
-            op("ve", lambda e: e.tensor_copy(out, src), r, [w])
-        else:
-            act(out, src, r, [w])
+    mates_mod(T.sv0[:, 0:19], reg("sv0"))
+    state_half(0, 0)
 
     for i, s in enumerate(STEP):
-        x, xn, na, lu, ll = "x%d" % i, "x%d" % (i + 1), "na%d" % i, "lu%d" % i, "ll%d" % i
+        x, xn, na, lp = "x%d" % i, "x%d" % (i + 1), "na%d" % i, "lp%d" % i
         qa, qp = "a%d" % i, "p%d" % i
         dst = T.cores[rank ^ s]
         rl = relays(topo, core, dst)
-        em = chip_masks(topo, core, rl)
-        ids = []
-        for k in rl:
-            rid, pid = topo.addr(k, core)
-            ids.append((rid, pid))
-        back = relays(topo, dst, core)
-        n_in = [len(topo.engines(k, core)) for k in back]
-        arrive(lu, n_in[0], [reg(lu)])
-        arrive("q" + qp, n_in[0], [reg("q" + qp)])
-        arrive(ll, n_in[1], [reg(ll)])
-        arrive("s" + qp, n_in[1], [reg("s" + qp)])
+        em = halves(topo, core, rl)
+        ids = [topo.addr(k, core) for k in rl]
+        n_in = [len(topo.engines(k, core)) for k in relays(topo, dst, core)]
+        arrive(lp, n_in[0], [reg(lp)])
+        arrive("s" + qp, n_in[0], [reg("s" + qp)])
+        arrive("q" + qp, n_in[1] + n_in[2], [reg("q" + qp)])
 
-        tt(T.fl[:, 0:H], T.scu[:], pv(5), A.is_gt, [reg("scu"), bank(5)], [reg("fl", 0, H)])
-        tt(T.fl[:, C:AW], T.scu[:], pv(5), A.is_le, [reg("scu"), bank(5)], [reg("fl", C, AW)])
-        tt(T.mgt[:], T.fl[:, 0:AW].indirect(T.lm[:, 0:28]), T.mskt[:], A.mult, [reg("fl"), reg("lm"), reg("mskt")], [reg("mgt")])
-        op("ve", lambda e: e.tensor_tensor_scan(T.sct[:], T.rst[:], T.mgt[:], 0.0, A.mult, A.add),
-           [reg("rst"), reg("mgt")], [reg("sct")])
-        tt(T.w1[:, 0:19], T.mm[:, 0:19], T.sct[:, 15:304:16], A.add, [reg("mm"), reg("sct")], [reg("w1")])
-        tt(T.d1[:, 0:9], T.w1[:, 10:19], T.w1[:, 0:9], A.subtract, [reg("w1")], [reg("d1")])
-        tt(T.e1[:, 0:9], T.d1[:, 0:9], T.sct[:, 319:448:16], A.mult, [reg("d1"), reg("sct")], [reg("e1")])
-        tt(T.nn[:, 0:9], T.w1[:, 0:9], T.e1[:, 0:9], A.add, [reg("w1"), reg("e1")], [reg("nn", 0, 9)])
-        tt(T.nn[:, 10:19], T.w1[:, 10:19], T.e1[:, 0:9], A.subtract, [reg("w1"), reg("e1")], [reg("nn", 10, 19)])
-        ts(T[na][:], T.nn[:], float(MID), None, A.add, None, [reg("nn")], [reg(na)])
-        sync("gp", [reg(na)], [])
-        g.remote_dma_fused([
-            RemoteDMATransfer(dst_ids=[DstId(rid=ids[0][0], pnc=ids[0][1])], dma_engine_mask=bits(em[0]),
-                              remote_sem=T.sem[lu], src=T[na][:, 0:10], dst=T[lu][:]),
-            RemoteDMATransfer(dst_ids=[DstId(rid=ids[1][0], pnc=ids[1][1])], dma_engine_mask=bits(em[1]),
-                              remote_sem=T.sem[ll], src=T[na][:, 10:20], dst=T[ll][:])], local_sem=T.sem.out)
-        outs[0] += len(em[0]) + len(em[1])
-        gather("ac", T.up[:, 0:H], "h", C, na, 10, 19, reg("up", 0, H))
+        def send(land, view, r, sem):
+            sync("gp", [r], [])
+            g.remote_dma(land, view, remote_sem=T.sem[sem], local_sem=T.sem.out, pid=ids[0][1], routing_id=ids[0][0],
+                         dma_engine_mask=topo.mask(core, rl[0]))
+            outs[0] += len(topo.engines(core, rl[0]))
 
-        def z_half(lo):
-            a, o = (H, 10) if lo else (0, 0)
-            for b in range(4):
-                tt(T.z[:, 4 * a + b:4 * (a + H):4], T.xp[:, C * b:C * b + C].indirect(T[na][:, o:o + 9]),
-                   T[x][:, 4 * a + b:4 * (a + H):4], A.add, [reg(x, a, a + H, b), reg("xp", C * b, C * b + C), reg(na, o, o + 9)],
-                   [reg("z", a, a + H, b)])
-            quant("qz", "sz", a, a + H, "z", a, a + H)
+        tt(T.fl[:, 0:H], pv(0), T.scl[:], A.is_gt, [reg("scl"), bank(0)], [reg("fl", 0, H)])
+        tt(T.fl[:, H:C], pv(0), T.scl[:], A.is_le, [reg("scl"), bank(0)], [reg("fl", H, C)])
+        pick(T.scf[:], reg("scf"), T.fl[:, 0:H], reg("fl", 0, H), "cf", H, 0.0)
+        ts(T.gt[:], T.fl[:].indirect(T.lm[:, 0:19]), float(OFF), None, A.add, None, [reg("fl"), reg("lm")], [reg("gt")])
+        pick(T.sct[:], reg("sct"), T.gt[:], reg("gt"), "ct", 304, 0.0)
+        hi, low = T.sct[:, 15:H:16], T.sct[:, 175:304:16]
+        tt(T.d1[:, 0:9], low, hi, A.subtract, [reg("sct")], [reg("d1")])
+        tt(T.e1[:, 0:9], T.d1[:, 0:9], T.scf[:, 15:H:16], A.mult, [reg("d1"), reg("scf")], [reg("e1")])
+        tt(T.nn[:, 0:9], low, T.e1[:, 0:9], A.add, [reg("sct"), reg("e1")], [reg("nn", 0, 9)])
+        tt(T.nn[:, 10:19], hi, T.e1[:, 0:9], A.subtract, [reg("sct"), reg("e1")], [reg("nn", 10, 19)])
+        ts(T[na][:], T.nn[:], float(TW), None, A.add, None, [reg("nn")], [reg(na)])
+        send(T[lp][:], T[na][:], reg(na), lp)
 
-        def a_half(lo):
-            a, k = (H, 0) if lo else (0, 4)
-            for b in range(4):
-                mul(k + b, "w", 128 * b, "z", a, a + H)
-            for b in range(4):
-                act(T.a[:, 4 * a + b:4 * (a + H):4], pv(k + b), [bank(k + b)], [reg("a", a, a + H, b)], scale=0.015625)
+        for b in range(4):
+            gather("ac", T.zg[:, b:4 * H:4], reg("zg", 0, H, b), "xp", C * b, C * b + C, na, 0)
+        for b in range(4):
+            tt(T.z[:, 4 * H + b:4 * C:4], T.xp[:, C * b:C * b + C].indirect(T[na][:, 10:19]), T[x][:, 4 * H + b:4 * C:4], A.add,
+               [reg(x, H, C, b), reg("xp", C * b, C * b + C), reg(na, 10, 19)], [reg("z", H, C, b)])
+        quant("qz", "sz", H, C, "z", H, C)
+        for b in range(4):
+            mul(b, "w", 128 * b, "z", H, C)
 
-        z_half(1)
-        a_half(1)
-        z_half(0)
-        a_half(0)
+        def a_copy(q, lo, b):
+            k = b if lo else 4 + b
+            cp(q, T.a[:, 4 * H * lo + b:4 * H * (lo + 1):4], pv(k), [bank(k)], [reg("a", H * lo, H * lo + H, b)], 0.015625)
+
+        gather("ac", T.up[:, 0:C:2], reg("up", 0, C, 0), "idt", 0, C, na, 10)
+        for b in range(4):
+            a_copy("ac", 1, b)
+        tt(T.z[:, 0:4 * H], T.zg[:], T[x][:, 0:4 * H], A.add, [reg("zg"), reg(x, 0, H)], [reg("z", 0, H)])
+        quant("qz", "sz", 0, H, "z", 0, H)
+        for b in range(4):
+            mul(4 + b, "w", 128 * b, "z", 0, H)
         quant("q" + qa, "s" + qa, H, C, "a", H, C)
-        for n, k, view in (("q", 0, T["q" + qa][:, H:C].bitcast(dt.uint8)), ("s", 1, T["s" + qa][:, H:C])):
-            sync("gp", [reg(n + qa, H, C)], [])
-            land = T[n + qp][:].bitcast(dt.uint8) if n == "q" else T[n + qp][:]
-            g.remote_dma(land, view, remote_sem=T.sem[n + qp], local_sem=T.sem.out, pid=ids[k][1], routing_id=ids[k][0],
-                         dma_engine_mask=bits(em[k]))
-            outs[0] += len(em[k])
+        sync("gp", [reg("q" + qa, H, C)], [])
+        g.remote_dma_fused([
+            RemoteDMATransfer(dst_ids=[DstId(rid=ids[1 + k][0], pnc=ids[1 + k][1])], dma_engine_mask=bits(em[k]),
+                              remote_sem=T.sem["q" + qp], src=code_half(T, "q" + qa, H, k), dst=code_half(T, "q" + qp, 0, k))
+            for k in range(2)], local_sem=T.sem.out)
+        outs[0] += len(em[0]) + len(em[1])
+        send(T["s" + qp][:], T["s" + qa][:, H:C], reg("s" + qa, H, C), "s" + qp)
         if i == 0:
-            ts(T.msk[:], T.ioa[:, 0:304], 0.0, None, A.is_equal, None, [reg("ioa", 0, 304)], [reg("msk")])
-            fill(T.et[:], 0.0, reg("et"))
+            gather("ac", T.cg[:], reg("cg"), "pat", 32, 48, "pl", 0, 9, float(BIG))
+            for t in ("up", "vtab"):
+                cp("ve", T[t][:, 1:C:2], T.idt[:, C:AW:2], [reg("idt")], [reg(t, 0, C, 1)])
+            for t in ("ta", "tb", "tc"):
+                cp("ve", T[t][:], T.idt[:], [reg("idt")], [reg(t)])
+            fill(T.scg[:, H:H + 16], float(-LOW), reg("scg", H, H + 16))
             for b in range(4):
-                op("ve", lambda e: e.tensor_copy(T.et[:, 513 * b:512 * b + 512:4], T.idn[:]), [reg("idn"), reg("et", 128 * b, 128 * b + 128)],
+                cp("ve", T.et[:, 513 * b:512 * b + 512:4], T.idn[:], [reg("idn"), reg("et", 128 * b, 128 * b + 128)],
                    [reg("et", 128 * b, 128 * b + 128, b)])
             op("ve", lambda e: e.quantize_mx(T.qe[:], T.se[:], T.et[:]), [reg("et")], [reg("qe"), reg("se")])
-        quant("q" + qa, "s" + qa, 0, H, "a", 0, H)
-        if i == 0:
             op("ve", lambda e: e.quantize_mx(T.qv[:], T.sv[:], T.vt[:]), [reg("vt")], [reg("qv"), reg("sv")])
-            for b in range(4):
-                fill(T.db[:, AW * b + H:AW * b + C], 0.0, reg("db", AW * b + H, AW * b + C))
+        for b in range(4):
+            a_copy("ac", 0, b)
+
+        def d_copy(q, lo, b):
+            k = 4 + b if lo else b
+            cp(q, T.db[:, C * b + H * lo:C * b + H * lo + H], pv(k), [bank(k)], [reg("db", C * b + H * lo, C * b + H * lo + H)])
+
+        def step(q, t, win, off):
+            v, w = nodes(t)
+            gather(q, v, w, win, 0, AW, off, 0)
+
+        def listed(t, lk):
+            v, r = nodes(t)
+            pick(T.sc[:], reg("sc"), v, r, "cg", H, float(-LOW))
+            ts(T[lk][:, 0:9], T.sc[:, 15:H:16], float(LOW), None, A.add, None, [reg("sc")], [reg(lk)])
+
+        v, w = nodes("ta")
+        gather("ve", v, w, "up", 0, C, lp, 0)
+        listed("ta", "lk0")
+        step("ve", "tb", "ta", "lk0")
+        quant("q" + qa, "s" + qa, 0, H, "a", 0, H)
         for b in range(4):
             mul(b, "e", 128 * b, qa, 0, H)
         for b in range(4):
-            act(T.db[:, AW * b:AW * b + H], pv(b), [bank(b)], [reg("db", AW * b, AW * b + H)])
-        for b in range(4):
             mul(4 + b, "e", 128 * b, qp, 0, H)
-
-        def table(t):
-            return T[t][:, H:C], reg(t, H, C)
-        mgu, mgl = (T.mg[:, 0:H], reg("mg", 0, H)), (T.mg[:, 160:304], reg("mg", 160, 304))
-        gather("ve", mgu[0], "up", C, lu, 0, 9, mgu[1], 0)
-        v, w = table("ta")
-        gather("ac", v, "up", C, lu, 0, 9, w)
-        spread(0, H, ("lk0", 9))
-        v, w = table("tb")
-        gather("ve", v, "ta", AW, "lk0", 0, 9, w)
-        now, lk = "tb", 0
-        for t in ("tc", "ta", "tb", "tc"):
-            gather("ve", mgu[0], now, AW, "lk%d" % lk, 0, 9, mgu[1], 0)
-            v, w = table(t)
-            gather("ac", v, now, AW, "lk%d" % lk, 0, 9, w)
-            lk = 1 - lk
-            spread(0, H, ("lk%d" % lk, 9))
-            now = t
-        for t in ("ta", "tb"):
-            v, w = table(t)
-            gather("ve", v, now, AW, "lk%d" % lk, 0, 9, w)
-            now = t
-        gather("ac", T.vtab[:, 0:H], now, AW, na, 10, 19, reg("vtab", 0, H))
-        gather("ve", mgu[0], now, AW, na, 0, 9, mgu[1], 0)
-        gather("ve", mgl[0], "vtab", C, ll, 0, 9, mgl[1], 160)
-        spread(0, 304, ("lm", 19))
+        step("ac", "tc", "tb", "lk0")
+        listed("tb", "lk1")
+        step("ve", "ta", "tc", "lk1")
+        step("ac", "tb", "ta", "lk1")
+        listed("ta", "lk0")
         for b in range(4):
-            act(T.db[:, AW * b + C:AW * b + AW], pv(4 + b), [bank(4 + b)], [reg("db", AW * b + C, AW * b + AW)])
-        if i + 1 == ROUNDS:
-            gather("ac", T.mrow[:], "gtb", AW, "lm", 0, 19, reg("mrow"))
-            dma("sy", T.mo[:, 0:H], T.mrow[0:128:16, 0:H], [reg("mrow")], [], "stm0")
-            dma("sy", T.mo[:, H:C], T.mrow[0:128:16, 160:304], [reg("mrow")], [], "stm1")
-        for lo in (0, 1):
+            d_copy("ac", 0, b)
+        step("ve", "tc", "tb", "lk0")
+        listed("tc", "lk1")
+        step("ve", "ta", "tc", "lk1")
+        listed("ta", "lk0")
+        step("ve", "tb", "ta", "lk0")
+        for b in range(2):
+            d_copy("ac", 1, b)
+        step("ve", "tc", "tb", "lk0")
+
+        def ends(lo, win, width, off):
             a, o = (H, 10) if lo else (0, 0)
-            for b in range(4):
-                tt(T[xn][:, 4 * a + b:4 * (a + H):4], T.db[:, AW * b:AW * b + AW].indirect(T.lm[:, o:o + 9]),
-                   T[x][:, 4 * a + b:4 * (a + H):4], A.add, [reg("db", AW * b, AW * b + AW), reg("lm", o, o + 9), reg(x, a, a + H, b)],
-                   [reg(xn, a, a + H, b)])
-            state_half(i + 1, lo)
+            gather("ve", T.fr[:, a:a + H], reg("fr", a, a + H), win, 0, width, off, o)
+
+        def ends_scan(lo):
+            a, c = (H, 160) if lo else (0, 0)
+            pick(T.scg[:, c:c + H], reg("scg", c, c + H), T.fr[:, a:a + H], reg("fr", a, a + H), "cg", H, float(-LOW))
+
+        def ends_list(lo):
+            c, o = (160, 10) if lo else (0, 0)
+            ts(T.lm[:, o:o + 9], T.scg[:, c + 15:c + H:16], float(LOW), 0.5, A.add, A.mult, [reg("scg", c, c + H)], [reg("lm", o, o + 9)])
+
+        gather("ac", T.vtab[:, 0:C:2], reg("vtab", 0, C, 0), "tc", 0, AW, na, 10)
+        for b in range(2, 4):
+            d_copy("ac", 1, b)
+        ends(0, "tc", AW, na)
+        ends_scan(0)
+        ends(1, "vtab", C, lp)
+        ends_list(0)
+        ends_scan(1)
+        ends_list(1)
+        for b in range(4):
+            gather("ac", T.dg[:, b:4 * H:4], reg("dg", 0, H, b), "db", C * b, C * b + C, "lm", 0)
+        for b in range(4):
+            tt(T[xn][:, 4 * H + b:4 * C:4], T.db[:, C * b:C * b + C].indirect(T.lm[:, 10:19]), T[x][:, 4 * H + b:4 * C:4], A.add,
+               [reg("db", C * b, C * b + C), reg("lm", 10, 19), reg(x, H, C, b)], [reg(xn, H, C, b)])
+        if i + 1 == ROUNDS:
+            op("ac", lambda e: e.activation(T.mrow[:], T.fr[:], copy, bias=float(MID // 2), scale=0.5), [reg("fr")], [reg("mrow")])
+            dma("sy", T.mo[:], T.mrow[0:128:16, :], [reg("mrow")], [], "stm")
+        state_half(i + 1, 1)
+        tt(T[xn][:, 0:4 * H], T.dg[:], T[x][:, 0:4 * H], A.add, [reg("dg"), reg(x, 0, H)], [reg(xn, 0, H)])
+        state_half(i + 1, 0)
         if i + 1 < ROUNDS:
-            sv = T.sc[:, 15:304:16]
-            ts(T.mt[:, 0:19], sv, 0.0, float(-C), A.is_ge, A.mult, [reg("sc")], [reg("mt")])
-            tt(T.mm[:, 0:19], T.mt[:, 0:19], sv, A.add, [reg("mt"), reg("sc")], [reg("mm")])
+            mates_mod(T.scg[:, 15:304:16], reg("scg"))
     for k in range(4):
-        dma("sy" if k % 2 else "ac", T.osc[4 * k:4 * k + 4, :], T.sx[32 * k:32 * k + 4, :], [reg("sx")], [], "sts%d" % k)
+        dma("sy", T.osc[4 * k:4 * k + 4, :], T.sx[32 * k:32 * k + 4, :], [reg("sx")], [], "sts%d" % k)
     for n in ("ve", "ac", "pe", "gp"):
         g.wait_ge(T.sem[n], count[n])
     for n in LOADS + STORES:

@@ -8,6 +8,7 @@ BIG = 576
 LOW = MID + BIG
 OFF, TW = 100, 188
 ROUNDS = len(STEP)
+CUT = 4
 
 SCRATCH = {}
 for _n in ("x0", "x1", "x2", "x3", "z", "a", "xp", "db"):
@@ -28,27 +29,27 @@ for _n in ("u", "r", "v"):
 for _n in ("w", "e"):
     SCRATCH["q" + _n] = ("sbuf", [128, 512], "float8_e4m3fn_x4")
     SCRATCH["s" + _n] = ("sbuf", [128, 512], "uint8")
-for _n in ("idt", "ta", "tb", "tc", "zg", "dg"):
+for _n in ("idt", "ta", "tb", "tc", "td", "zg", "dg"):
     SCRATCH[_n] = ("sbuf", [128, AW], "bfloat16")
-for _n in ("up", "vtab", "fl", "fr"):
+for _n in ("up", "vtab", "fl", "fr", "fs", "gt", "sct", "scf", "ct"):
     SCRATCH[_n] = ("sbuf", [128, C], "bfloat16")
-for _n in ("sv0", "mt", "mu", "d1", "e1", "nn"):
-    SCRATCH[_n] = ("sbuf", [128, 20], "float32")
+for _n in ("mt", "mu"):
+    SCRATCH[_n] = ("sbuf", [128, 18], "float32")
+for _n in ("cs", "nn"):
+    SCRATCH[_n] = ("sbuf", [128, 40], "float32")
+for _n in ("lm", "lt", "ls"):
+    SCRATCH[_n] = ("sbuf", [128, 20], "uint16")
+for _n in ("scg", "scs"):
+    SCRATCH[_n] = ("sbuf", [128, C], "float16")
 SCRATCH.update({
     "et": ("sbuf", [128, 2048], "bfloat16"),
     "ones": ("sbuf", [128, 128], "bfloat16"),
     "idn": ("sbuf", [128, 128], "bfloat16"),
     "mli": ("sbuf", [128, 18], "int32"),
-    "lm": ("sbuf", [128, 20], "uint16"),
     "scl": ("sbuf", [128, H], "float32"),
-    "gt": ("sbuf", [128, 304], "bfloat16"),
-    "sct": ("sbuf", [128, 304], "bfloat16"),
-    "scf": ("sbuf", [128, H], "bfloat16"),
-    "ct": ("sbuf", [128, 304], "bfloat16"),
     "cf": ("sbuf", [128, H], "bfloat16"),
     "cg": ("sbuf", [128, H], "bfloat16"),
     "sc": ("sbuf", [128, H], "float16"),
-    "scg": ("sbuf", [128, 304], "float16"),
     "lk0": ("sbuf", [128, 10], "uint16"),
     "lk1": ("sbuf", [128, 10], "uint16"),
     "mrow": ("sbuf", [128, C], "float32"),
@@ -62,7 +63,7 @@ SCRATCH.update({
     "c0": ("sbuf", [128, 1], "float32"),
     "col": ("sbuf", [128, 48], "float32"),
     "eq": ("sbuf", [128, 48], "float32"),
-    "lt": ("sbuf", [128, 48], "float32"),
+    "bf": ("sbuf", [128, 48], "float32"),
     "pat": ("sbuf", [128, 48], "bfloat16"),
     "ps": ("psum", [128, 4096], "float32"),
 })
@@ -217,19 +218,16 @@ def rank_program(g, core, T, topo):
     def tt(out, in0, in1, o, r, w):
         op("ve", lambda e: e.tensor_tensor(out, in0, in1, o), r, w)
 
-    def act(out, in_, r, w, scale=None):
-        if scale is None:
-            op("ac", lambda e: e.activation(out, in_, copy), r, w)
-        else:
-            op("ac", lambda e: e.activation(out, in_, copy, scale=scale), r, w)
-
-    def cp(q, out, in_, r, w, scale=None):
+    def cp(q, out, in_, r, w, scale=None, bias=None):
         if q == "ac":
-            act(out, in_, r, w, scale)
-        elif scale is None:
-            op("ve", lambda e: e.tensor_copy(out, in_), r, w)
-        else:
+            kw = {k: v for k, v in (("scale", scale), ("bias", bias)) if v is not None}
+            op("ac", lambda e: e.activation(out, in_, copy, **kw), r, w)
+        elif scale is not None:
             ts(out, in_, scale, None, A.mult, None, r, w)
+        elif bias is not None:
+            ts(out, in_, bias, None, A.add, None, r, w)
+        else:
+            op("ve", lambda e: e.tensor_copy(out, in_), r, w)
 
     def quant(qn, sn, a, b, tile, ta, tb):
         op("ve", lambda e: e.quantize_mx(T[qn][:, a:b], T[sn][:, a:b], T[tile][:, 4 * ta:4 * tb]),
@@ -250,20 +248,22 @@ def rank_program(g, core, T, topo):
     def pv(k):
         return T.ps[:, 512 * k:512 * k + H]
 
-    def gather(q, out, w, win, a, b, off, o, n=9, scale=None):
-        cp(q, out, T[win][:, a:b].indirect(T[off][:, o:o + n]), [reg(win, a, b), reg(off, o, o + n)], [w], scale)
+    def gather(q, out, w, win, a, b, off, o, n=9, scale=None, bias=None):
+        cp(q, out, T[win][:, a:b].indirect(T[off][:, o:o + n]), [reg(win, a, b), reg(off, o, o + n)], [w], scale, bias)
 
-    def pick(out, w, data, r, const, n, start):
-        op("ve", lambda e: e.tensor_tensor_scan(out, data, T[const][:, 0:n], start, A.max, A.add), [r, reg(const)], [w])
+    def part(q, t, first, step, win, width, off, o, k0, k1):
+        a, b = first + 16 * step * k0, first + 16 * step * k1 - step + 1
+        gather(q, T[t][:, a:b:step], reg(t, a, b, first % step if step > 1 else None), win, 0, width, off, o + k0, k1 - k0)
 
-    def nodes(t):
-        return T[t][:, 1:C:2], reg(t, 0, C, 1)
+    def pick(t, a, data, r, const, n, start):
+        op("ve", lambda e: e.tensor_tensor_scan(T[t][:, a:a + n], data, T[const][:, 0:n], start, A.max, A.add),
+           [r, reg(const)], [reg(t, a, a + n)])
 
-    dma("ac", T.ut[:], T.u[:], [], [reg("ut")], "ldu")
+    dma("sy", T.ut[:], T.u[:], [], [reg("ut")], "ldu")
+    dma("ac", T.mli[:], T.ml[:], [], [reg("mli")], "ldm")
     dma("sy", T.x0[:, 576:1152], T.x[:, 576:1152], [], [reg("x0", H, C)], "ldxl")
     dma("sy", T.x0[:, 0:576], T.x[:, 0:576], [], [reg("x0", 0, H)], "ldxu")
-    dma("ac", T.mli[:], T.ml[:], [], [reg("mli")], "ldm")
-    dma("sy", T.qw[:].bitcast(dt.uint8), T.wc[:], [], [reg("qw")], "ldw")
+    dma("sy", T.qw[:].bitcast(dt.uint8), T.wc[:], [reg("x0", H, C)], [reg("qw")], "ldw")
     dma("sy", T.sw[:], T.ws[:], [], [reg("sw")], "lds")
     dma("sy", T.vt[:], T.v[:], [], [reg("vt")], "ldv")
 
@@ -272,33 +272,41 @@ def rank_program(g, core, T, topo):
     iota(T.ul[:], [[16, 8]], 0, 0, reg("ul"))
     iota(T.idt[:], [[1, AW]], -MID, 0, reg("idt"), True)
     fill(T.ones[:], 1.0, reg("ones"))
-    fill(T.lm[:], 0, reg("lm"))
-    fill(T.nn[:], float(-TW), reg("nn"))
-    fill(T.sv0[:], float(-LOW), reg("sv0"))
+    fill(T.nn[:], float(C - TW), reg("nn"))
     ts(T.pd[:], T.pc[:], 15, None, A.bitwise_and, None, [reg("pc")], [reg("pd")])
     cp("ve", T.pm[:], T.pd[:, 0:1], [reg("pd")], [reg("pm")])
     cp("ve", T.pl[:], T.pd[:], [reg("pd")], [reg("pl")])
     ts(T.eq[:], T.col[:], T.pm[:], None, A.is_equal, None, [reg("col"), reg("pm")], [reg("eq")])
-    ts(T.lt[:], T.col[:], T.pm[:], None, A.is_lt, None, [reg("col"), reg("pm")], [reg("lt")])
+    ts(T.bf[:], T.col[:], T.pm[:], None, A.is_lt, None, [reg("col"), reg("pm")], [reg("bf")])
     cp("ve", T.uo[:], T.ul[:], [reg("ul")], [reg("uo")])
-    tt(T.pat[:], T.eq[:], T.lt[:], A.subtract, [reg("eq"), reg("lt")], [reg("pat")])
-    ts(T.c0[:], T.eq[:, 15:16], 2.0, float(LOW - 290), A.mult, A.add, [reg("eq")], [reg("c0")])
+    tt(T.pat[:], T.eq[:], T.bf[:], A.subtract, [reg("eq"), reg("bf")], [reg("pat")])
+    ts(T.c0[:], T.eq[:, 15:16], 2.0, float(-C - 2), A.mult, A.add, [reg("eq")], [reg("c0")])
     ts(T.pat[:, 31:32], T.eq[:, 15:16], -1.5, None, A.add, None, [reg("eq")], [reg("pat", 31, 32)])
     ts(T.pat[:, 47:48], T.eq[:, 15:16], -2.0, None, A.add, None, [reg("eq")], [reg("pat", 47, 48)])
-    gather("ac", T.ct[:], reg("ct"), "pat", 0, 16, "pl", 0, 19, 2.0)
+    gather("ac", T.ct[:], reg("ct"), "pat", 0, 16, "pl", 0, 18, 2.0)
     gather("ac", T.cf[:], reg("cf"), "pat", 16, 32, "pl", 0, 9, 2.0)
     op("gp", lambda e: e.affine_select(T.idn[:], T.ones[:], [[-1, 128]], A.is_equal, 0.0, 0, 1), [reg("ones")], [reg("idn")])
-    fill(T.et[:], 0.0, reg("et"))
+    fill(T.et[:, 0:1024], 0.0, reg("et", 0, 256))
 
+    def turn_list(lo, view, r, s1, s2, o0, o1):
+        ts(T.lt[:, lo:18:2], view, s1, s2, o0, o1, [r], [reg("lt", 0, 18, lo)])
+
+    def mates_mod():
+        ts(T.mt[:], T.lt[:, 0:18], float(H), float(-C), A.is_ge, A.mult, [reg("lt")], [reg("mt")])
+        ts(T.mu[:], T.lt[:, 0:18], 2.0, T.c0[:], A.mult, A.add, [reg("lt"), reg("c0")], [reg("mu")])
+        tt(T.ct[:, 15:C:16], T.mt[:], T.mu[:], A.add, [reg("mt"), reg("mu")], [reg("ct")])
+
+    for lo in (0, 1):
+        turn_list(lo, T.mli[:, 9 * lo:9 * lo + 9], reg("mli"), 0.0, None, A.add, None)
+    mates_mod()
     op("ve", lambda e: e.quantize_mx(T.qu[:], T.su[:], T.ut[:]), [reg("ut")], [reg("qu"), reg("su")])
     op("ve", lambda e: e.tensor_copy(T.qr[:, 0:128].bitcast(dt.uint32), T.qu[:, 0:128].bitcast(dt.uint32).indirect(T.uo[:, 0:8])),
        [reg("qu"), reg("uo")], [reg("qr")])
-    act(T.sr[:, 0:128], T.su[:, 0:128].indirect(T.uo[:, 0:8]), [reg("su"), reg("uo")], [reg("sr")])
+    cp("ac", T.sr[:, 0:128], T.su[:, 0:128].indirect(T.uo[:, 0:8]), [reg("su"), reg("uo")], [reg("sr")])
 
-    def planes(k, lo):
-        for b in range(4):
-            act(T.xp[:, C * b + lo:C * b + C:2], T["x%d" % k][:, 4 * H * lo + b:4 * H * (lo + 1):4],
-                [reg("x%d" % k, H * lo, H * lo + H, b)], [reg("xp", C * b, C * b + C, lo)])
+    def plane(k, lo, b):
+        cp("ac", T.xp[:, C * b + lo:C * b + C:2], T["x%d" % k][:, 4 * H * lo + b:4 * H * (lo + 1):4],
+           [reg("x%d" % k, H * lo, H * lo + H, b)], [reg("xp", C * b, C * b + C, lo)])
 
     def state_half(k, lo):
         a = H * lo
@@ -306,24 +314,21 @@ def rank_program(g, core, T, topo):
         if k < ROUNDS:
             mul(lo, "r", 0, "x", a, a + H)
             if lo:
-                act(T.scl[:], pv(1), [bank(1)], [reg("scl")])
-            planes(k, lo)
+                plane(k, 1, 0)
+                plane(k, 1, 1)
+                cp("ac", T.scl[:], pv(1), [bank(1)], [reg("scl")])
+                plane(k, 1, 2)
+                plane(k, 1, 3)
+            else:
+                plane(k, 0, 0)
+                plane(k, 0, 1)
         else:
             dma("sy", T.oc[:, 4 * a:4 * a + 4 * H], T.qx[:, a:a + H].bitcast(dt.uint8), [reg("qx", a, a + H)], [], "stc%d" % lo)
             mul(lo, "v", 0, "x", a, a + H)
-            act(T.ys[:, a:a + H], pv(lo), [bank(lo)], [reg("ys", a, a + H)])
+            cp("ac", T.ys[:, a:a + H], pv(lo), [bank(lo)], [reg("ys", a, a + H)])
             dma("ac", T.y[:, a:a + H], T.ys[:, a:a + H], [reg("ys", a, a + H)], [], "sty%d" % lo)
 
-    def mates_mod(sv, r):
-        ts(T.mt[:, 0:19], sv, float(C - LOW), float(-C), A.is_ge, A.mult, [r], [reg("mt")])
-        ts(T.mu[:, 0:19], sv, T.c0[:], None, A.add, None, [r, reg("c0")], [reg("mu")])
-        tt(T.ct[:, 15:304:16], T.mt[:, 0:19], T.mu[:, 0:19], A.add, [reg("mt"), reg("mu")], [reg("ct")])
-
-    for a, b in ((0, 0), (10, 9)):
-        cp("ve", T.lm[:, a:a + 9], T.mli[:, b:b + 9], [reg("mli")], [reg("lm", a, a + 9)])
-        ts(T.sv0[:, a:a + 9], T.mli[:, b:b + 9], 2.0, float(-LOW), A.mult, A.add, [reg("mli")], [reg("sv0", a, a + 9)])
     state_half(0, 1)
-    mates_mod(T.sv0[:, 0:19], reg("sv0"))
     state_half(0, 0)
 
     for i, s in enumerate(STEP):
@@ -346,15 +351,20 @@ def rank_program(g, core, T, topo):
 
         tt(T.fl[:, 0:H], pv(0), T.scl[:], A.is_gt, [reg("scl"), bank(0)], [reg("fl", 0, H)])
         tt(T.fl[:, H:C], pv(0), T.scl[:], A.is_le, [reg("scl"), bank(0)], [reg("fl", H, C)])
-        pick(T.scf[:], reg("scf"), T.fl[:, 0:H], reg("fl", 0, H), "cf", H, 0.0)
-        ts(T.gt[:], T.fl[:].indirect(T.lm[:, 0:19]), float(OFF), None, A.add, None, [reg("fl"), reg("lm")], [reg("gt")])
-        pick(T.sct[:], reg("sct"), T.gt[:], reg("gt"), "ct", 304, 0.0)
-        hi, low = T.sct[:, 15:H:16], T.sct[:, 175:304:16]
-        tt(T.d1[:, 0:9], low, hi, A.subtract, [reg("sct")], [reg("d1")])
-        tt(T.e1[:, 0:9], T.d1[:, 0:9], T.scf[:, 15:H:16], A.mult, [reg("d1"), reg("scf")], [reg("e1")])
-        tt(T.nn[:, 0:9], low, T.e1[:, 0:9], A.add, [reg("sct"), reg("e1")], [reg("nn", 0, 9)])
-        tt(T.nn[:, 10:19], hi, T.e1[:, 0:9], A.subtract, [reg("sct"), reg("e1")], [reg("nn", 10, 19)])
-        ts(T[na][:], T.nn[:], float(TW), None, A.add, None, [reg("nn")], [reg(na)])
+        for a in (0, H):
+            pick("scf", a, T.fl[:, a:a + H], reg("fl", a, a + H), "cf", H, 0.0)
+        for q, k0, k1 in (("ac", 0, 10), ("ve", 10, 18)):
+            gather(q, T.gt[:, 16 * k0:16 * k1], reg("gt", 16 * k0, 16 * k1), "fl", 0, C, "lt", k0, k1 - k0, bias=float(OFF))
+        plane(i, 0, 2)
+        plane(i, 0, 3)
+        ts(T.cs[:, 0:36:2], T.scf[:, 15:C:16], -2.0 * C, float(-C), A.mult, A.add, [reg("scf")], [reg("cs", 0, 36, 0)])
+        ts(T.cs[:, 1:36:2], T.scf[:, 15:C:16], float(C), float(-C), A.mult, A.add, [reg("scf")], [reg("cs", 0, 36, 1)])
+        pick("sct", 0, T.gt[:], reg("gt"), "ct", C, 0.0)
+        for lo in (0, 1):
+            op("ve", lambda e: e.tensor_tensor_scan(T.nn[:, 20 * lo:20 * lo + 18], T.sct[:, 15:C:16], T.cs[:, 18 * lo:18 * lo + 18],
+                                                    float(-C - TW), A.max, A.add),
+               [reg("sct"), reg("cs")], [reg("nn", 20 * lo, 20 * lo + 18)])
+        cp("ve", T[na][:], T.nn[:, 1:40:2], [reg("nn")], [reg(na)], bias=float(C + TW))
         send(T[lp][:], T[na][:], reg(na), lp)
 
         for b in range(4):
@@ -370,11 +380,19 @@ def rank_program(g, core, T, topo):
             k = b if lo else 4 + b
             cp(q, T.a[:, 4 * H * lo + b:4 * H * (lo + 1):4], pv(k), [bank(k)], [reg("a", H * lo, H * lo + H, b)], 0.015625)
 
-        gather("ac", T.up[:, 0:C:2], reg("up", 0, C, 0), "idt", 0, C, na, 10)
-        for b in range(4):
-            a_copy("ac", 1, b)
-        tt(T.z[:, 0:4 * H], T.zg[:], T[x][:, 0:4 * H], A.add, [reg("zg"), reg(x, 0, H)], [reg("z", 0, H)])
+        def add_upper(out, got, k):
+            a, b = k * H // 2, (k + 1) * H // 2
+            tt(T[out][:, 4 * a:4 * b], T[got][:, 4 * a:4 * b], T[x][:, 4 * a:4 * b], A.add, [reg(got, a, b), reg(x, a, b)],
+               [reg(out, a, b)])
+
+        part("ac", "up", 0, 2, "idt", C, na, 10, 0, 9)
+        a_copy("ac", 1, 0)
+        a_copy("ac", 1, 2)
+        add_upper("z", "zg", 0)
+        add_upper("z", "zg", 1)
+        a_copy("ve", 1, 1)
         quant("qz", "sz", 0, H, "z", 0, H)
+        a_copy("ve", 1, 3)
         for b in range(4):
             mul(4 + b, "w", 128 * b, "z", 0, H)
         quant("q" + qa, "s" + qa, H, C, "a", H, C)
@@ -387,11 +405,11 @@ def rank_program(g, core, T, topo):
         send(T["s" + qp][:], T["s" + qa][:, H:C], reg("s" + qa, H, C), "s" + qp)
         if i == 0:
             gather("ac", T.cg[:], reg("cg"), "pat", 32, 48, "pl", 0, 9, float(BIG))
+            fill(T.et[:, 1024:2048], 0.0, reg("et", 256, 512))
             for t in ("up", "vtab"):
                 cp("ve", T[t][:, 1:C:2], T.idt[:, C:AW:2], [reg("idt")], [reg(t, 0, C, 1)])
-            for t in ("ta", "tb", "tc"):
+            for t in ("ta", "tb", "tc", "td"):
                 cp("ve", T[t][:], T.idt[:], [reg("idt")], [reg(t)])
-            fill(T.scg[:, H:H + 16], float(-LOW), reg("scg", H, H + 16))
             for b in range(4):
                 cp("ve", T.et[:, 513 * b:512 * b + 512:4], T.idn[:], [reg("idn"), reg("et", 128 * b, 128 * b + 128)],
                    [reg("et", 128 * b, 128 * b + 128, b)])
@@ -404,74 +422,84 @@ def rank_program(g, core, T, topo):
             k = 4 + b if lo else b
             cp(q, T.db[:, C * b + H * lo:C * b + H * lo + H], pv(k), [bank(k)], [reg("db", C * b + H * lo, C * b + H * lo + H)])
 
-        def step(q, t, win, off):
-            v, w = nodes(t)
-            gather(q, v, w, win, 0, AW, off, 0)
+        def own_d():
+            quant("q" + qa, "s" + qa, 0, H, "a", 0, H)
+            for b in range(4):
+                mul(b, "e", 128 * b, qa, 0, H)
+            for b in range(4):
+                mul(4 + b, "e", 128 * b, qp, 0, H)
+
+        def to_list(out, o, t, a, step=1, half=None):
+            ts(T[out][:, o:o + 9 * step - step + 1:step], T[t][:, a + 15:a + H:16], float(LOW), half, A.add,
+               None if half is None else A.mult, [reg(t, a, a + H)],
+               [reg(out, o, o + 9) if step == 1 else reg(out, 0, 18, o)])
+
+        spare = [None, None, own_d,
+                 lambda: part("ve", "fs", 0, 1, "tb", AW, na, 0, 0, CUT), lambda: part("ve", "fs", 0, 1, "tb", AW, na, 0, CUT, 9),
+                 lambda: part("ve", "vtab", 0, 2, "tb", AW, na, 10, 0, CUT),
+                 lambda: part("ve", "vtab", 0, 2, "tb", AW, na, 10, CUT, 9), lambda: d_copy("ve", 0, 0), lambda: d_copy("ve", 0, 1),
+                 lambda: part("ve", "fs", H, 1, "vtab", C, lp, 10, 0, CUT), lambda: part("ve", "fs", H, 1, "vtab", C, lp, 10, CUT, 9),
+                 lambda: d_copy("ve", 0, 2),
+                 lambda: [pick("scs", a, T.fs[:, a:a + H], reg("fs", a, a + H), "cg", H, float(-LOW)) for a in (0, H)],
+                 lambda: [to_list("ls", o, "scs", a) for o, a in ((0, 0), (10, H))], lambda: d_copy("ve", 0, 3),
+                 None]
+
+        def gap():
+            f = spare.pop(0)
+            if f is not None:
+                f()
+
+        def shared(t, win, lk):
+            part("ac", t, 1, 2, win, AW, lk, 0, 0, CUT)
+            part("ve", t, 1, 2, win, AW, lk, 0, CUT, 9)
 
         def listed(t, lk):
-            v, r = nodes(t)
-            pick(T.sc[:], reg("sc"), v, r, "cg", H, float(-LOW))
-            ts(T[lk][:, 0:9], T.sc[:, 15:H:16], float(LOW), None, A.add, None, [reg("sc")], [reg(lk)])
+            gap()
+            pick("sc", 0, T[t][:, 1:C:2], reg(t, 0, C, 1), "cg", H, float(-LOW))
+            gap()
+            to_list(lk, 0, "sc", 0)
+            gap()
 
-        v, w = nodes("ta")
-        gather("ve", v, w, "up", 0, C, lp, 0)
+        part("ve", "ta", 1, 2, "up", C, lp, 0, 0, 9)
         listed("ta", "lk0")
-        step("ve", "tb", "ta", "lk0")
-        quant("q" + qa, "s" + qa, 0, H, "a", 0, H)
-        for b in range(4):
-            mul(b, "e", 128 * b, qa, 0, H)
-        for b in range(4):
-            mul(4 + b, "e", 128 * b, qp, 0, H)
-        step("ac", "tc", "tb", "lk0")
-        listed("tb", "lk1")
-        step("ve", "ta", "tc", "lk1")
-        step("ac", "tb", "ta", "lk1")
-        listed("ta", "lk0")
-        for b in range(4):
-            d_copy("ac", 0, b)
-        step("ve", "tc", "tb", "lk0")
-        listed("tc", "lk1")
-        step("ve", "ta", "tc", "lk1")
-        listed("ta", "lk0")
-        step("ve", "tb", "ta", "lk0")
+        now, lk = "ta", 0
+        for t, more in (("tb", "tc"), ("ta", "td"), ("tc", "ta"), ("td", "tc")):
+            shared(t, now, "lk%d" % lk)
+            part("ac", more, 1, 2, t, AW, "lk%d" % lk, 0, 0, 9)
+            now, lk = more, 1 - lk
+            listed(t, "lk%d" % lk)
+        shared("ta", now, "lk%d" % lk)
+        gap()
+        part("ve", "fr", 0, 1, "ta", AW, "ls", 0, 0, 9)
+        part("ac", "fr", H, 1, "ta", AW, "ls", 10, 0, 9)
         for b in range(2):
             d_copy("ac", 1, b)
-        step("ve", "tc", "tb", "lk0")
-
-        def ends(lo, win, width, off):
-            a, o = (H, 10) if lo else (0, 0)
-            gather("ve", T.fr[:, a:a + H], reg("fr", a, a + H), win, 0, width, off, o)
-
-        def ends_scan(lo):
-            a, c = (H, 160) if lo else (0, 0)
-            pick(T.scg[:, c:c + H], reg("scg", c, c + H), T.fr[:, a:a + H], reg("fr", a, a + H), "cg", H, float(-LOW))
-
-        def ends_list(lo):
-            c, o = (160, 10) if lo else (0, 0)
-            ts(T.lm[:, o:o + 9], T.scg[:, c + 15:c + H:16], float(LOW), 0.5, A.add, A.mult, [reg("scg", c, c + H)], [reg("lm", o, o + 9)])
-
-        gather("ac", T.vtab[:, 0:C:2], reg("vtab", 0, C, 0), "tc", 0, AW, na, 10)
-        for b in range(2, 4):
-            d_copy("ac", 1, b)
-        ends(0, "tc", AW, na)
-        ends_scan(0)
-        ends(1, "vtab", C, lp)
-        ends_list(0)
-        ends_scan(1)
-        ends_list(1)
+        d_copy("ve", 1, 2)
+        for a in (0, H):
+            pick("scg", a, T.fr[:, a:a + H], reg("fr", a, a + H), "cg", H, float(-LOW))
+        for o, a in ((0, 0), (10, H)):
+            to_list("lm", o, "scg", a, half=0.5)
+        d_copy("ve", 1, 3)
         for b in range(4):
             gather("ac", T.dg[:, b:4 * H:4], reg("dg", 0, H, b), "db", C * b, C * b + C, "lm", 0)
         for b in range(4):
             tt(T[xn][:, 4 * H + b:4 * C:4], T.db[:, C * b:C * b + C].indirect(T.lm[:, 10:19]), T[x][:, 4 * H + b:4 * C:4], A.add,
                [reg("db", C * b, C * b + C), reg("lm", 10, 19), reg(x, H, C, b)], [reg(xn, H, C, b)])
-        if i + 1 == ROUNDS:
-            op("ac", lambda e: e.activation(T.mrow[:], T.fr[:], copy, bias=float(MID // 2), scale=0.5), [reg("fr")], [reg("mrow")])
+        last = i + 1 == ROUNDS
+        if last:
+            cp("ac", T.mrow[:], T.fr[:], [reg("fr")], [reg("mrow")], 0.5, float(MID // 2))
             dma("sy", T.mo[:], T.mrow[0:128:16, :], [reg("mrow")], [], "stm")
+        if not last:
+            for lo in (0, 1):
+                to_list("lt", lo, "scg", H * lo, 2, 0.5)
+            add_upper(xn, "dg", 0)
         state_half(i + 1, 1)
-        tt(T[xn][:, 0:4 * H], T.dg[:], T[x][:, 0:4 * H], A.add, [reg("dg"), reg(x, 0, H)], [reg(xn, 0, H)])
+        if last:
+            add_upper(xn, "dg", 0)
+        add_upper(xn, "dg", 1)
         state_half(i + 1, 0)
-        if i + 1 < ROUNDS:
-            mates_mod(T.scg[:, 15:304:16], reg("scg"))
+        if not last:
+            mates_mod()
     for k in range(4):
         dma("sy", T.osc[4 * k:4 * k + 4, :], T.sx[32 * k:32 * k + 4, :], [reg("sx")], [], "sts%d" % k)
     for n in ("ve", "ac", "pe", "gp"):

@@ -29,9 +29,13 @@ for _n in ("u", "r", "v"):
 for _n in ("w", "e"):
     SCRATCH["q" + _n] = ("sbuf", [128, 512], "float8_e4m3fn_x4")
     SCRATCH["s" + _n] = ("sbuf", [128, 512], "uint8")
-for _n in ("idt", "ta", "tb", "tc", "td", "zg", "dg"):
+for _n in ("idt", "ta", "tb", "tc", "zg", "dg"):
     SCRATCH[_n] = ("sbuf", [128, AW], "bfloat16")
-for _n in ("up", "vtab", "fl", "fr", "fs", "gt", "sct", "scf", "ct"):
+SCRATCH["mp"] = ("sbuf", [128, 18], "int32")
+SCRATCH["m0"] = ("sbuf", [128, 20], "uint16")
+for _n in ("tp", "t0"):
+    SCRATCH[_n] = ("sbuf", [128, 10], "uint16")
+for _n in ("up", "upx", "g1", "g2", "vtab", "fl", "fr", "fs", "gt", "sct", "scf", "ct"):
     SCRATCH[_n] = ("sbuf", [128, C], "bfloat16")
 for _n in ("mt", "mu"):
     SCRATCH[_n] = ("sbuf", [128, 18], "float32")
@@ -42,9 +46,10 @@ for _n in ("lm", "lt", "ls"):
 for _n in ("scg", "scs"):
     SCRATCH[_n] = ("sbuf", [128, C], "float16")
 SCRATCH.update({
-    "et": ("sbuf", [128, 2048], "bfloat16"),
-    "ones": ("sbuf", [128, 128], "bfloat16"),
-    "idn": ("sbuf", [128, 128], "bfloat16"),
+    "et": ("sbuf", [128, 516], "bfloat16"),
+    "ones": ("sbuf", [128, AW], "bfloat16"),
+    "cu": ("sbuf", [128, H], "bfloat16"),
+    "c1": ("sbuf", [128, 1], "float32"),
     "mli": ("sbuf", [128, 18], "int32"),
     "scl": ("sbuf", [128, H], "float32"),
     "cf": ("sbuf", [128, H], "bfloat16"),
@@ -54,7 +59,6 @@ SCRATCH.update({
     "lk1": ("sbuf", [128, 10], "uint16"),
     "mrow": ("sbuf", [128, C], "float32"),
     "ys": ("sbuf", [128, C], "float32"),
-    "ul": ("sbuf", [128, 8], "int32"),
     "uo": ("sbuf", [128, 8], "uint16"),
     "pc": ("sbuf", [128, 20], "int32"),
     "pd": ("sbuf", [128, 20], "int32"),
@@ -69,7 +73,7 @@ SCRATCH.update({
 })
 LOADS = ["ldxu", "ldxl", "ldu", "ldm", "ldw", "lds", "ldv"]
 STORES = ["sty0", "sty1", "stc0", "stc1", "sts0", "sts1", "sts2", "sts3", "stm"]
-SEMAPHORES = (["ve", "ac", "pe", "gp", "out"] + LOADS + STORES
+SEMAPHORES = (["ve", "ac", "pe", "gp", "out", "mp", "tp"] + LOADS + STORES
               + [n + "%d" % i for n in ("lp", "qp", "sp") for i in range(ROUNDS)])
 
 
@@ -84,11 +88,15 @@ def bits(es):
     return sum(1 << e for e in es)
 
 
-def halves(topo, src, rl):
-    e = topo.engines(src, rl[1])
-    f = topo.engines(src, rl[2])
+def halves(topo, src, two):
+    e = topo.engines(src, two[0])
+    f = topo.engines(src, two[1])
     n = len(e) // 2
     return [e[:n], [k for k in f if k not in e[:n]][:n]]
+
+
+def list_relay(i):
+    return 0 if i else 2
 
 
 def code_half(T, name, first, k):
@@ -110,10 +118,18 @@ def relay_program(g, core, T, topo):
             continue
         role = rl.index(core)
         rid, pid = topo.addr(dst, core)
+        every = len(topo.engines(src, core))
+        jobs = []
+        if i == 0 and role < 2:
+            jobs.append(("mp", T.mp[:, 9 * role:9 * role + 9], len(halves(topo, src, rl[:2])[role])))
+        if i == 0 and role == 0:
+            jobs.append(("tp", T.tp[:], every))
+        if role == list_relay(i):
+            jobs.append(("lp%d" % i, T["lp%d" % i][:], every))
         if role == 0:
-            jobs = [(n + "%d" % i, T[n + "%d" % i][:], len(topo.engines(src, core))) for n in ("lp", "sp")]
+            jobs.append(("sp%d" % i, T["sp%d" % i][:], every))
         else:
-            jobs = [("qp%d" % i, code_half(T, "qp%d" % i, 0, role - 1), len(halves(topo, src, rl)[role - 1]))]
+            jobs.append(("qp%d" % i, code_half(T, "qp%d" % i, 0, role - 1), len(halves(topo, src, rl[1:])[role - 1])))
         for sem, ap, got in jobs:
             g.wait_ge(T.sem[sem], got)
             g.remote_dma(ap, ap, remote_sem=T.sem[sem], local_sem=T.sem.out, pid=pid, routing_id=rid,
@@ -263,30 +279,61 @@ def rank_program(g, core, T, topo):
     dma("ac", T.mli[:], T.ml[:], [], [reg("mli")], "ldm")
     dma("sy", T.x0[:, 576:1152], T.x[:, 576:1152], [], [reg("x0", H, C)], "ldxl")
     dma("sy", T.x0[:, 0:576], T.x[:, 0:576], [], [reg("x0", 0, H)], "ldxu")
-    dma("sy", T.qw[:].bitcast(dt.uint8), T.wc[:], [reg("x0", H, C)], [reg("qw")], "ldw")
+    dma("sy", T.qw[:].bitcast(dt.uint8), T.wc[:], [reg("ut")], [reg("qw")], "ldw")
     dma("sy", T.sw[:], T.ws[:], [], [reg("sw")], "lds")
-    dma("sy", T.vt[:], T.v[:], [], [reg("vt")], "ldv")
 
     iota(T.pc[:], [[0, 20]], 0, 1, reg("pc"))
     iota(T.col[:], [[0, 3], [1, 16]], 0, 0, reg("col"), True)
-    iota(T.ul[:], [[16, 8]], 0, 0, reg("ul"))
-    iota(T.idt[:], [[1, AW]], -MID, 0, reg("idt"), True)
     fill(T.ones[:], 1.0, reg("ones"))
     fill(T.nn[:], float(C - TW), reg("nn"))
+    fill(T.t0[:], 0, reg("t0"))
+    op("gp", lambda e: e.affine_select(T.et[:], T.ones[:, 0:516], [[-1, 516]], A.is_equal, 0.0, 3, 4), [reg("ones")], [reg("et")])
     ts(T.pd[:], T.pc[:], 15, None, A.bitwise_and, None, [reg("pc")], [reg("pd")])
+    op("ve", lambda e: e.tensor_tensor_scan(T.idt[:], T.ones[:], T.ones[:], float(-MID - 1), A.mult, A.add), [reg("ones")], [reg("idt")])
     cp("ve", T.pm[:], T.pd[:, 0:1], [reg("pd")], [reg("pm")])
     cp("ve", T.pl[:], T.pd[:], [reg("pd")], [reg("pl")])
     ts(T.eq[:], T.col[:], T.pm[:], None, A.is_equal, None, [reg("col"), reg("pm")], [reg("eq")])
     ts(T.bf[:], T.col[:], T.pm[:], None, A.is_lt, None, [reg("col"), reg("pm")], [reg("bf")])
-    cp("ve", T.uo[:], T.ul[:], [reg("ul")], [reg("uo")])
     tt(T.pat[:], T.eq[:], T.bf[:], A.subtract, [reg("eq"), reg("bf")], [reg("pat")])
     ts(T.c0[:], T.eq[:, 15:16], 2.0, float(-C - 2), A.mult, A.add, [reg("eq")], [reg("c0")])
     ts(T.pat[:, 31:32], T.eq[:, 15:16], -1.5, None, A.add, None, [reg("eq")], [reg("pat", 31, 32)])
     ts(T.pat[:, 47:48], T.eq[:, 15:16], -2.0, None, A.add, None, [reg("eq")], [reg("pat", 47, 48)])
+    ts(T.c1[:], T.pm[:], 2.0, T.c0[:], A.mult, A.add, [reg("pm"), reg("c0")], [reg("c1")])
     gather("ac", T.ct[:], reg("ct"), "pat", 0, 16, "pl", 0, 18, 2.0)
     gather("ac", T.cf[:], reg("cf"), "pat", 16, 32, "pl", 0, 9, 2.0)
-    op("gp", lambda e: e.affine_select(T.idn[:], T.ones[:], [[-1, 128]], A.is_equal, 0.0, 0, 1), [reg("ones")], [reg("idn")])
-    fill(T.et[:, 0:1024], 0.0, reg("et", 0, 256))
+
+    def ways(i):
+        dst = T.cores[rank ^ STEP[i]]
+        rl = relays(topo, core, dst)
+        return rl, [topo.addr(k, core) for k in rl], [len(topo.engines(k, core)) for k in relays(topo, dst, core)]
+
+    def send(i, land, view, r, k=0):
+        rl, ids, _ = ways(i)
+        sync("gp", [r], [])
+        g.remote_dma(T[land][:], view, remote_sem=T.sem[land], local_sem=T.sem.out, pid=ids[k][1], routing_id=ids[k][0],
+                     dma_engine_mask=topo.mask(core, rl[k]))
+        outs[0] += len(topo.engines(core, rl[k]))
+
+    def send_two(i, land, pairs, r, k):
+        rl, ids, _ = ways(i)
+        em = halves(topo, core, rl[k:k + 2])
+        sync("gp", [r], [])
+        g.remote_dma_fused([
+            RemoteDMATransfer(dst_ids=[DstId(rid=ids[k + j][0], pnc=ids[k + j][1])], dma_engine_mask=bits(em[j]),
+                              remote_sem=T.sem[land], src=pairs[j][0], dst=pairs[j][1]) for j in range(2)], local_sem=T.sem.out)
+        outs[0] += len(em[0]) + len(em[1])
+
+    def places(t):
+        iota(T[t][:], [[1, AW]], -MID, 0, reg(t), True)
+
+    def far_ends(t, k):
+        cp("ve", T[t][:, k:C:2], T.idt[:, C:AW:2], [reg("idt")], [reg(t, 0, C, k)])
+
+    send_two(0, "mp", [(T.mli[:, a:a + 9], T.mp[:, a:a + 9]) for a in (0, 9)], reg("mli"), 0)
+
+    def unit(b):
+        op("ve", lambda e: e.quantize_mx(T.qe[:, 128 * b:128 * b + 128], T.se[:, 128 * b:128 * b + 128], T.et[:, 3 - b:515 - b]),
+           [reg("et")], [reg("qe", 128 * b, 128 * b + 128), reg("se", 128 * b, 128 * b + 128)])
 
     def turn_list(lo, view, r, s1, s2, o0, o1):
         ts(T.lt[:, lo:18:2], view, s1, s2, o0, o1, [r], [reg("lt", 0, 18, lo)])
@@ -296,10 +343,10 @@ def rank_program(g, core, T, topo):
         ts(T.mu[:], T.lt[:, 0:18], 2.0, T.c0[:], A.mult, A.add, [reg("lt"), reg("c0")], [reg("mu")])
         tt(T.ct[:, 15:C:16], T.mt[:], T.mu[:], A.add, [reg("mt"), reg("mu")], [reg("ct")])
 
+    cp("ve", T.uo[:], T.idt[:, MID:MID + 128:16], [reg("idt")], [reg("uo")], bias=0.0)
+    op("ve", lambda e: e.quantize_mx(T.qu[:], T.su[:], T.ut[:]), [reg("ut")], [reg("qu"), reg("su")])
     for lo in (0, 1):
         turn_list(lo, T.mli[:, 9 * lo:9 * lo + 9], reg("mli"), 0.0, None, A.add, None)
-    mates_mod()
-    op("ve", lambda e: e.quantize_mx(T.qu[:], T.su[:], T.ut[:]), [reg("ut")], [reg("qu"), reg("su")])
     op("ve", lambda e: e.tensor_copy(T.qr[:, 0:128].bitcast(dt.uint32), T.qu[:, 0:128].bitcast(dt.uint32).indirect(T.uo[:, 0:8])),
        [reg("qu"), reg("uo")], [reg("qr")])
     cp("ac", T.sr[:, 0:128], T.su[:, 0:128].indirect(T.uo[:, 0:8]), [reg("su"), reg("uo")], [reg("sr")])
@@ -314,11 +361,12 @@ def rank_program(g, core, T, topo):
         if k < ROUNDS:
             mul(lo, "r", 0, "x", a, a + H)
             if lo:
-                plane(k, 1, 0)
-                plane(k, 1, 1)
+                early = 4 if k else 2
+                for b in range(early):
+                    plane(k, 1, b)
                 cp("ac", T.scl[:], pv(1), [bank(1)], [reg("scl")])
-                plane(k, 1, 2)
-                plane(k, 1, 3)
+                for b in range(early, 4):
+                    plane(k, 1, b)
             else:
                 plane(k, 0, 0)
                 plane(k, 0, 1)
@@ -329,30 +377,32 @@ def rank_program(g, core, T, topo):
             dma("ac", T.y[:, a:a + H], T.ys[:, a:a + H], [reg("ys", a, a + H)], [], "sty%d" % lo)
 
     state_half(0, 1)
+    cp("ve", T.cu[:], T.cf[:], [reg("cf")], [reg("cu")])
+    mates_mod()
     state_half(0, 0)
+    ts(T.cu[:, 15:H:16], T.idt[:, MID:MID + C:32], T.c1[:], None, A.add, None, [reg("idt"), reg("c1")], [reg("cu")])
+    cp("ve", T.ta[:], T.idt[:], [reg("idt")], [reg("ta")])
 
     for i, s in enumerate(STEP):
         x, xn, na, lp = "x%d" % i, "x%d" % (i + 1), "na%d" % i, "lp%d" % i
         qa, qp = "a%d" % i, "p%d" % i
-        dst = T.cores[rank ^ s]
-        rl = relays(topo, core, dst)
-        em = halves(topo, core, rl)
-        ids = [topo.addr(k, core) for k in rl]
-        n_in = [len(topo.engines(k, core)) for k in relays(topo, dst, core)]
-        arrive(lp, n_in[0], [reg(lp)])
+        n_in = ways(i)[2]
+        if i == 0:
+            arrive("mp", n_in[0] + n_in[1], [reg("mp")])
+            arrive("tp", n_in[0], [reg("tp")])
+        arrive(lp, n_in[list_relay(i)], [reg(lp)])
         arrive("s" + qp, n_in[0], [reg("s" + qp)])
         arrive("q" + qp, n_in[1] + n_in[2], [reg("q" + qp)])
 
-        def send(land, view, r, sem):
-            sync("gp", [r], [])
-            g.remote_dma(land, view, remote_sem=T.sem[sem], local_sem=T.sem.out, pid=ids[0][1], routing_id=ids[0][0],
-                         dma_engine_mask=topo.mask(core, rl[0]))
-            outs[0] += len(topo.engines(core, rl[0]))
-
         tt(T.fl[:, 0:H], pv(0), T.scl[:], A.is_gt, [reg("scl"), bank(0)], [reg("fl", 0, H)])
         tt(T.fl[:, H:C], pv(0), T.scl[:], A.is_le, [reg("scl"), bank(0)], [reg("fl", H, C)])
+        if i == 0:
+            pick("sc", 0, T.fl[:, 0:H], reg("fl", 0, H), "cu", H, 0.0)
         for a in (0, H):
             pick("scf", a, T.fl[:, a:a + H], reg("fl", a, a + H), "cf", H, 0.0)
+        if i == 0:
+            cp("ve", T.t0[:, 0:9], T.sc[:, 15:H:16], [reg("sc")], [reg("t0")], bias=float(C))
+            send(0, "tp", T.t0[:], reg("t0"))
         for q, k0, k1 in (("ac", 0, 10), ("ve", 10, 18)):
             gather(q, T.gt[:, 16 * k0:16 * k1], reg("gt", 16 * k0, 16 * k1), "fl", 0, C, "lt", k0, k1 - k0, bias=float(OFF))
         plane(i, 0, 2)
@@ -360,21 +410,36 @@ def rank_program(g, core, T, topo):
         ts(T.cs[:, 0:36:2], T.scf[:, 15:C:16], -2.0 * C, float(-C), A.mult, A.add, [reg("scf")], [reg("cs", 0, 36, 0)])
         ts(T.cs[:, 1:36:2], T.scf[:, 15:C:16], float(C), float(-C), A.mult, A.add, [reg("scf")], [reg("cs", 0, 36, 1)])
         pick("sct", 0, T.gt[:], reg("gt"), "ct", C, 0.0)
+        if i == 0:
+            far_ends("up", 1)
+            far_ends("upx", 0)
         for lo in (0, 1):
             op("ve", lambda e: e.tensor_tensor_scan(T.nn[:, 20 * lo:20 * lo + 18], T.sct[:, 15:C:16], T.cs[:, 18 * lo:18 * lo + 18],
                                                     float(-C - TW), A.max, A.add),
                [reg("sct"), reg("cs")], [reg("nn", 20 * lo, 20 * lo + 18)])
+        if i == 0:
+            far_ends("vtab", 1)
         cp("ve", T[na][:], T.nn[:, 1:40:2], [reg("nn")], [reg(na)], bias=float(C + TW))
-        send(T[lp][:], T[na][:], reg(na), lp)
+        send(i, lp, T[na][:], reg(na), list_relay(i))
+        if i == 0:
+            places("tb")
+            places("tc")
+            gather("ac", T.cg[:], reg("cg"), "pat", 32, 48, "pl", 0, 9, float(BIG))
+            unit(2)
 
         for b in range(4):
             gather("ac", T.zg[:, b:4 * H:4], reg("zg", 0, H, b), "xp", C * b, C * b + C, na, 0)
         for b in range(4):
             tt(T.z[:, 4 * H + b:4 * C:4], T.xp[:, C * b:C * b + C].indirect(T[na][:, 10:19]), T[x][:, 4 * H + b:4 * C:4], A.add,
                [reg(x, H, C, b), reg("xp", C * b, C * b + C), reg(na, 10, 19)], [reg("z", H, C, b)])
+        if i == 0:
+            unit(3)
         quant("qz", "sz", H, C, "z", H, C)
         for b in range(4):
             mul(b, "w", 128 * b, "z", H, C)
+        part("ac", "up", 0, 2, "idt", C, na, 10, 0, 9)
+        if i == 0:
+            part("ac", "upx", 1, 2, "idt", C, na, 10, 0, 9)
 
         def a_copy(q, lo, b):
             k = b if lo else 4 + b
@@ -385,7 +450,6 @@ def rank_program(g, core, T, topo):
             tt(T[out][:, 4 * a:4 * b], T[got][:, 4 * a:4 * b], T[x][:, 4 * a:4 * b], A.add, [reg(got, a, b), reg(x, a, b)],
                [reg(out, a, b)])
 
-        part("ac", "up", 0, 2, "idt", C, na, 10, 0, 9)
         a_copy("ac", 1, 0)
         a_copy("ac", 1, 2)
         add_upper("z", "zg", 0)
@@ -395,27 +459,24 @@ def rank_program(g, core, T, topo):
         a_copy("ve", 1, 3)
         for b in range(4):
             mul(4 + b, "w", 128 * b, "z", 0, H)
-        quant("q" + qa, "s" + qa, H, C, "a", H, C)
-        sync("gp", [reg("q" + qa, H, C)], [])
-        g.remote_dma_fused([
-            RemoteDMATransfer(dst_ids=[DstId(rid=ids[1 + k][0], pnc=ids[1 + k][1])], dma_engine_mask=bits(em[k]),
-                              remote_sem=T.sem["q" + qp], src=code_half(T, "q" + qa, H, k), dst=code_half(T, "q" + qp, 0, k))
-            for k in range(2)], local_sem=T.sem.out)
-        outs[0] += len(em[0]) + len(em[1])
-        send(T["s" + qp][:], T["s" + qa][:, H:C], reg("s" + qa, H, C), "s" + qp)
         if i == 0:
-            gather("ac", T.cg[:], reg("cg"), "pat", 32, 48, "pl", 0, 9, float(BIG))
-            fill(T.et[:, 1024:2048], 0.0, reg("et", 256, 512))
-            for t in ("up", "vtab"):
-                cp("ve", T[t][:, 1:C:2], T.idt[:, C:AW:2], [reg("idt")], [reg(t, 0, C, 1)])
-            for t in ("ta", "tb", "tc", "td"):
-                cp("ve", T[t][:], T.idt[:], [reg("idt")], [reg(t)])
-            for b in range(4):
-                cp("ve", T.et[:, 513 * b:512 * b + 512:4], T.idn[:], [reg("idn"), reg("et", 128 * b, 128 * b + 128)],
-                   [reg("et", 128 * b, 128 * b + 128, b)])
-            op("ve", lambda e: e.quantize_mx(T.qe[:], T.se[:], T.et[:]), [reg("et")], [reg("qe"), reg("se")])
+            for lo in (0, 1):
+                cp("ve", T.m0[:, 10 * lo:10 * lo + 9], T.mp[:, 9 * lo:9 * lo + 9], [reg("mp")], [reg("m0", 10 * lo, 10 * lo + 9)])
+        quant("q" + qa, "s" + qa, H, C, "a", H, C)
+        send_two(i, "q" + qp, [(code_half(T, "q" + qa, H, k), code_half(T, "q" + qp, 0, k)) for k in range(2)],
+                 reg("q" + qa, H, C), 1)
+        send(i, "s" + qp, T["s" + qa][:, H:C], reg("s" + qa, H, C))
+        if i == 0:
+            part("ac", "g1", 0, 1, "up", C, "tp", 0, 0, 9)
+            part("ve", "g1", H, 1, "upx", C, "tp", 0, 0, 9)
+            unit(0)
+            a_copy("ac", 0, 0)
+            part("ac", "g2", 0, 2, "g1", C, "m0", 0, 0, 9)
+            part("ve", "g2", 1, 2, "g1", C, "m0", 10, 0, 9)
+            unit(1)
+        if i == 1:
             op("ve", lambda e: e.quantize_mx(T.qv[:], T.sv[:], T.vt[:]), [reg("vt")], [reg("qv"), reg("sv")])
-        for b in range(4):
+        for b in range(0 if i else 1, 4):
             a_copy("ac", 0, b)
 
         def d_copy(q, lo, b):
@@ -460,18 +521,20 @@ def rank_program(g, core, T, topo):
             to_list(lk, 0, "sc", 0)
             gap()
 
-        part("ve", "ta", 1, 2, "up", C, lp, 0, 0, 9)
+        part("ve", "ta", 1, 2, "up" if i else "g2", C, lp if i else "tp", 0, 0, 9)
         listed("ta", "lk0")
+        if i == 0:
+            dma("sy", T.vt[:], T.v[:], [reg("g2")], [reg("vt")], "ldv")
         now, lk = "ta", 0
-        for t, more in (("tb", "tc"), ("ta", "td"), ("tc", "ta"), ("td", "tc")):
+        for t, more in (("tb", "tc"), ("ta", "tc"), ("ta", "tb"), ("tc", "ta")):
             shared(t, now, "lk%d" % lk)
             part("ac", more, 1, 2, t, AW, "lk%d" % lk, 0, 0, 9)
             now, lk = more, 1 - lk
             listed(t, "lk%d" % lk)
-        shared("ta", now, "lk%d" % lk)
+        shared("tb", now, "lk%d" % lk)
         gap()
-        part("ve", "fr", 0, 1, "ta", AW, "ls", 0, 0, 9)
-        part("ac", "fr", H, 1, "ta", AW, "ls", 10, 0, 9)
+        part("ve", "fr", 0, 1, "tb", AW, "ls", 0, 0, 9)
+        part("ac", "fr", H, 1, "tb", AW, "ls", 10, 0, 9)
         for b in range(2):
             d_copy("ac", 1, b)
         d_copy("ve", 1, 2)
@@ -489,14 +552,19 @@ def rank_program(g, core, T, topo):
         if last:
             cp("ac", T.mrow[:], T.fr[:], [reg("fr")], [reg("mrow")], 0.5, float(MID // 2))
             dma("sy", T.mo[:], T.mrow[0:128:16, :], [reg("mrow")], [], "stm")
+
+        def add_plane(b):
+            tt(T[xn][:, b:4 * H:4], T.dg[:, b:4 * H:4], T[x][:, b:4 * H:4], A.add, [reg("dg", 0, H, b), reg(x, 0, H, b)],
+               [reg(xn, 0, H, b)])
+        early = 1 if last else 3
+        for b in range(early):
+            add_plane(b)
+        state_half(i + 1, 1)
+        for b in range(early, 4):
+            add_plane(b)
         if not last:
             for lo in (0, 1):
                 to_list("lt", lo, "scg", H * lo, 2, 0.5)
-            add_upper(xn, "dg", 0)
-        state_half(i + 1, 1)
-        if last:
-            add_upper(xn, "dg", 0)
-        add_upper(xn, "dg", 1)
         state_half(i + 1, 0)
         if not last:
             mates_mod()

from concourse.bass import DstId, RemoteDMATransfer
from concourse.mybir import dt, AluOpType, ActivationFunctionType

C, H = 288, 144
STEP = (4, 1, 2)
AW, MID = 576, 144
BIG = 576
LOW = MID + BIG
OFF, TW = 100, 188
ROUNDS = len(STEP)
CUT = 4

SCRATCH = {}
for _n in ("x0", "x1", "x2", "x3", "z", "a", "xp", "db"):
    SCRATCH[_n] = ("sbuf", [128, 4 * C], "bfloat16")
for _n in ["x", "z"] + ["a%d" % i for i in range(ROUNDS)]:
    SCRATCH["q" + _n] = ("sbuf", [128, C], "float8_e4m3fn_x4")
    SCRATCH["s" + _n] = ("sbuf", [128, C], "uint8")
for _n in range(ROUNDS):
    SCRATCH["qp%d" % _n] = ("sbuf", [128, H], "float8_e4m3fn_x4")
    SCRATCH["sp%d" % _n] = ("sbuf", [128, H], "uint8")
    SCRATCH["lp%d" % _n] = ("sbuf", [128, 20], "uint16")
    SCRATCH["na%d" % _n] = ("sbuf", [128, 20], "uint16")
for _n in ("u", "v"):
    SCRATCH[_n + "t"] = ("sbuf", [128, 512], "bfloat16")
for _n in ("u", "r", "v"):
    SCRATCH["q" + _n] = ("sbuf", [128, 128], "float8_e4m3fn_x4")
    SCRATCH["s" + _n] = ("sbuf", [128, 128], "uint8")
for _n in ("w", "e"):
    SCRATCH["q" + _n] = ("sbuf", [128, 512], "float8_e4m3fn_x4")
    SCRATCH["s" + _n] = ("sbuf", [128, 512], "uint8")
for _n in ("idt", "ta", "tb", "tc", "zg", "dg"):
    SCRATCH[_n] = ("sbuf", [128, AW], "bfloat16")
SCRATCH["mp"] = ("sbuf", [128, 18], "int32")
SCRATCH["m0"] = ("sbuf", [128, 20], "uint16")
for _n in ("tp", "t0"):
    SCRATCH[_n] = ("sbuf", [128, 10], "uint16")
for _n in ("up", "upx", "g1", "g2", "vtab", "fl", "fr", "fs", "gt", "sct", "scf", "ct"):
    SCRATCH[_n] = ("sbuf", [128, C], "bfloat16")
for _n in ("mt", "mu"):
    SCRATCH[_n] = ("sbuf", [128, 18], "float32")
for _n in ("cs", "nn"):
    SCRATCH[_n] = ("sbuf", [128, 40], "float32")
for _n in ("lm", "lt", "ls"):
    SCRATCH[_n] = ("sbuf", [128, 20], "uint16")
for _n in ("scg", "scs"):
    SCRATCH[_n] = ("sbuf", [128, C], "float16")
SCRATCH.update({
    "et": ("sbuf", [128, 516], "bfloat16"),
    "ones": ("sbuf", [128, AW], "bfloat16"),
    "cu": ("sbuf", [128, H], "bfloat16"),
    "c1": ("sbuf", [128, 1], "float32"),
    "mli": ("sbuf", [128, 18], "int32"),
    "scl": ("sbuf", [128, H], "float32"),
    "cf": ("sbuf", [128, H], "bfloat16"),
    "cg": ("sbuf", [128, H], "bfloat16"),
    "sc": ("sbuf", [128, H], "float16"),
    "lk0": ("sbuf", [128, 10], "uint16"),
    "lk1": ("sbuf", [128, 10], "uint16"),
    "mrow": ("sbuf", [128, C], "float32"),
    "ys": ("sbuf", [128, C], "float32"),
    "uo": ("sbuf", [128, 8], "uint16"),
    "pc": ("sbuf", [128, 20], "int32"),
    "pd": ("sbuf", [128, 20], "int32"),
    "pl": ("sbuf", [128, 20], "uint16"),
    "pm": ("sbuf", [128, 1], "float32"),
    "c0": ("sbuf", [128, 1], "float32"),
    "col": ("sbuf", [128, 48], "float32"),
    "eq": ("sbuf", [128, 48], "float32"),
    "bf": ("sbuf", [128, 48], "float32"),
    "pat": ("sbuf", [128, 48], "bfloat16"),
    "ps": ("psum", [128, 4096], "float32"),
})
LOADS = ["ldxu", "ldxl", "ldu", "ldm", "ldw", "lds", "ldv"]
STORES = ["sty0", "sty1", "stc0", "stc1", "sts0", "sts1", "sts2", "sts3", "stm"]
SEMAPHORES = (["ve", "ac", "pe", "gp", "out", "mp", "tp"] + LOADS + STORES
              + [n + "%d" % i for n in ("lp", "qp", "sp") for i in range(ROUNDS)])


def relays(topo, src, dst):
    ks = [k for k in topo.cores_of(src) if k != src and topo.may_write(k, dst)]
    near = [k for k in ks if topo.die(k) == topo.die(src)]
    far = [k for k in ks if topo.die(k) != topo.die(src)]
    return [near[0], near[1], far[0]]


def bits(es):
    return sum(1 << e for e in es)


def halves(topo, src, two):
    e = topo.engines(src, two[0])
    f = topo.engines(src, two[1])
    n = len(e) // 2
    return [e[:n], [k for k in f if k not in e[:n]][:n]]


def list_relay(i):
    return 0 if i else 2


def code_half(T, name, first, k):
    a = first + k * H // 2
    return T[name][:, a:a + H // 2].bitcast(dt.uint8)


def relay_program(g, core, T, topo):
    home = [r for r, c in enumerate(T.cores) if core in topo.cores_of(c)]
    if not home:
        return
    r = home[0]
    src = T.cores[r]
    sent = 0
    for i, s in enumerate(STEP):
        dst = T.cores[r ^ s]
        rl = relays(topo, src, dst)
        if core not in rl:
            continue
        role = rl.index(core)
        rid, pid = topo.addr(dst, core)
        every = len(topo.engines(src, core))
        jobs = []
        if i == 0 and role < 2:
            jobs.append(("mp", T.mp[:, 9 * role:9 * role + 9], len(halves(topo, src, rl[:2])[role])))
        if i == 0 and role == 0:
            jobs.append(("tp", T.tp[:], every))
        if role == list_relay(i):
            jobs.append(("lp%d" % i, T["lp%d" % i][:], every))
        if role == 0:
            jobs.append(("sp%d" % i, T["sp%d" % i][:], every))
        else:
            jobs.append(("qp%d" % i, code_half(T, "qp%d" % i, 0, role - 1), len(halves(topo, src, rl[1:])[role - 1])))
        for sem, ap, got in jobs:
            g.wait_ge(T.sem[sem], got)
            g.remote_dma(ap, ap, remote_sem=T.sem[sem], local_sem=T.sem.out, pid=pid, routing_id=rid,
                         dma_engine_mask=topo.mask(core, dst))
            sent += len(topo.engines(core, dst))
    if sent:
        g.wait_ge(T.sem.out, sent)


def tracker(g, T):
    queues = {"ve": g.vector, "ac": g.scalar, "pe": g.tensor, "gp": g, "sy": g.sync}
    clock = {q: {} for q in queues}
    count = {q: 0 for q in queues}
    snap, acc = {}, {}

    def sync(q, reads, writes):
        req = {}
        for rw, regs in (("r", reads), ("w", writes)):
            for buf, a, b, lane in regs:
                for rw2, a2, b2, lane2, prod, cnt in acc.get(buf, []):
                    if a2 >= b or a >= b2 or (lane is not None and lane2 is not None and lane != lane2):
                        continue
                    if rw == "r" and rw2 == "r" and (buf != "ps" or prod == q):
                        continue
                    req[prod] = max(req.get(prod, 0), cnt)
        for p, n in req.items():
            if clock[q].get(p, 0) >= n:
                continue
            if any(p2 != p and snap[(p2, n2)].get(p, 0) >= n for p2, n2 in req.items()):
                continue
            queues[q].wait_ge(T.sem[p], n)
            for k, x in snap[(p, n)].items():
                clock[q][k] = max(clock[q].get(k, 0), x)

        for p, n in req.items():
            clock[q][p] = max(clock[q].get(p, 0), n)

    def note(prod, cnt, reads, writes):
        for rw, regs in (("r", reads), ("w", writes)):
            for buf, a, b, lane in regs:
                old = acc.get(buf, [])
                if rw == "w":
                    old = [o for o in old if not (a <= o[1] and o[2] <= b and (lane is None or lane == o[3]))]
                else:
                    old = [o for o in old if not (o[0] == "r" and o[4] == prod and a <= o[1] and o[2] <= b
                                                  and (lane is None or lane == o[3]))]
                acc[buf] = old + [(rw, a, b, lane, prod, cnt)]

    def op(q, fn, reads, writes):
        sync(q, reads, writes)
        count[q] += 1
        fn(queues[q]).then_inc(T.sem[q], 1)
        s = dict(clock[q])
        s[q] = count[q]
        snap[(q, count[q])] = s
        note(q, count[q], reads, writes)

    def dma(q, out, in_, reads, writes, sem):
        sync(q, reads, writes)
        queues[q].dma_start(out, in_).then_inc(T.sem[sem], 16)
        s = dict(clock[q])
        s[sem] = 16
        snap[(sem, 16)] = s
        note(sem, 16, reads, writes)

    def arrive(sem, n, writes):
        snap[(sem, n)] = {sem: n}
        note(sem, n, [], writes)

    return op, dma, arrive, sync, count


def reg(buf, a=None, b=None, lane=None):
    return (buf, 0 if a is None else a, 1 << 20 if b is None else b, lane)


def rank_program(g, core, T, topo):
    rank = T.rank_of(core)
    if rank is None:
        relay_program(g, core, T, topo)
        return
    op, dma, arrive, sync, count = tracker(g, T)
    A = AluOpType
    copy = ActivationFunctionType.Copy
    outs = [0]

    def fill(view, value, w):
        op("ve", lambda e: e.memset(view, value), [], [w])

    def iota(view, pattern, base, cm, w, small=False):
        if small:
            op("gp", lambda e: e.iota(view, pattern, base, cm, allow_small_or_imprecise_dtypes=True), [], [w])
        else:
            op("gp", lambda e: e.iota(view, pattern, base, cm), [], [w])

    def ts(out, in0, s1, s2, op0, op1, r, w):
        if op1 is None:
            op("ve", lambda e: e.tensor_scalar(out, in0, s1, None, op0), r, w)
        else:
            op("ve", lambda e: e.tensor_scalar(out, in0, s1, s2, op0, op1), r, w)

    def tt(out, in0, in1, o, r, w):
        op("ve", lambda e: e.tensor_tensor(out, in0, in1, o), r, w)

    def cp(q, out, in_, r, w, scale=None, bias=None):
        if q == "ac":
            kw = {k: v for k, v in (("scale", scale), ("bias", bias)) if v is not None}
            op("ac", lambda e: e.activation(out, in_, copy, **kw), r, w)
        elif scale is not None:
            ts(out, in_, scale, None, A.mult, None, r, w)
        elif bias is not None:
            ts(out, in_, bias, None, A.add, None, r, w)
        else:
            op("ve", lambda e: e.tensor_copy(out, in_), r, w)

    def quant(qn, sn, a, b, tile, ta, tb):
        op("ve", lambda e: e.quantize_mx(T[qn][:, a:b], T[sn][:, a:b], T[tile][:, 4 * ta:4 * tb]),
           [reg(tile, ta, tb)], [reg(qn, a, b), reg(sn, a, b)])

    def mul(bank, st, s0, mv, m0, m1):
        qs, ss = "q" + st, "s" + st
        qm, sm = "q" + mv, "s" + mv
        n = m1 - m0
        op("pe", lambda e: e.matmul_mx(T.ps[:, 512 * bank:512 * bank + n], T[qs][:, s0:s0 + 128], T[ss][:, s0:s0 + 128],
                                       T[qm][:, m0:m1], T[sm][:, m0:m1], True, True),
           [reg(qs, s0, s0 + 128), reg(ss, s0, s0 + 128), reg(qm, m0, m1), reg(sm, m0, m1)],
           [reg("ps", 512 * bank, 512 * bank + 512)])

    def bank(k):
        return reg("ps", 512 * k, 512 * k + 512)

    def pv(k):
        return T.ps[:, 512 * k:512 * k + H]

    def gather(q, out, w, win, a, b, off, o, n=9, scale=None, bias=None):
        cp(q, out, T[win][:, a:b].indirect(T[off][:, o:o + n]), [reg(win, a, b), reg(off, o, o + n)], [w], scale, bias)

    def part(q, t, first, step, win, width, off, o, k0, k1):
        a, b = first + 16 * step * k0, first + 16 * step * k1 - step + 1
        gather(q, T[t][:, a:b:step], reg(t, a, b, first % step if step > 1 else None), win, 0, width, off, o + k0, k1 - k0)

    def pick(t, a, data, r, const, n, start):
        op("ve", lambda e: e.tensor_tensor_scan(T[t][:, a:a + n], data, T[const][:, 0:n], start, A.max, A.add),
           [r, reg(const)], [reg(t, a, a + n)])

    dma("sy", T.ut[:], T.u[:], [], [reg("ut")], "ldu")
    dma("ac", T.mli[:], T.ml[:], [], [reg("mli")], "ldm")
    dma("sy", T.x0[:, 576:1152], T.x[:, 576:1152], [], [reg("x0", H, C)], "ldxl")
    dma("sy", T.x0[:, 0:576], T.x[:, 0:576], [], [reg("x0", 0, H)], "ldxu")
    dma("sy", T.qw[:].bitcast(dt.uint8), T.wc[:], [reg("ut")], [reg("qw")], "ldw")
    dma("sy", T.sw[:], T.ws[:], [], [reg("sw")], "lds")

    iota(T.pc[:], [[0, 20]], 0, 1, reg("pc"))
    iota(T.col[:], [[0, 3], [1, 16]], 0, 0, reg("col"), True)
    fill(T.ones[:], 1.0, reg("ones"))
    fill(T.nn[:], float(C - TW), reg("nn"))
    fill(T.t0[:], 0, reg("t0"))
    op("gp", lambda e: e.affine_select(T.et[:], T.ones[:, 0:516], [[-1, 516]], A.is_equal, 0.0, 3, 4), [reg("ones")], [reg("et")])
    ts(T.pd[:], T.pc[:], 15, None, A.bitwise_and, None, [reg("pc")], [reg("pd")])
    op("ve", lambda e: e.tensor_tensor_scan(T.idt[:], T.ones[:], T.ones[:], float(-MID - 1), A.mult, A.add), [reg("ones")], [reg("idt")])
    cp("ve", T.pm[:], T.pd[:, 0:1], [reg("pd")], [reg("pm")])
    cp("ve", T.pl[:], T.pd[:], [reg("pd")], [reg("pl")])
    ts(T.eq[:], T.col[:], T.pm[:], None, A.is_equal, None, [reg("col"), reg("pm")], [reg("eq")])
    ts(T.bf[:], T.col[:], T.pm[:], None, A.is_lt, None, [reg("col"), reg("pm")], [reg("bf")])
    tt(T.pat[:], T.eq[:], T.bf[:], A.subtract, [reg("eq"), reg("bf")], [reg("pat")])
    ts(T.c0[:], T.eq[:, 15:16], 2.0, float(-C - 2), A.mult, A.add, [reg("eq")], [reg("c0")])
    ts(T.pat[:, 31:32], T.eq[:, 15:16], -1.5, None, A.add, None, [reg("eq")], [reg("pat", 31, 32)])
    ts(T.pat[:, 47:48], T.eq[:, 15:16], -2.0, None, A.add, None, [reg("eq")], [reg("pat", 47, 48)])
    ts(T.c1[:], T.pm[:], 2.0, T.c0[:], A.mult, A.add, [reg("pm"), reg("c0")], [reg("c1")])
    gather("ac", T.ct[:], reg("ct"), "pat", 0, 16, "pl", 0, 18, 2.0)
    gather("ac", T.cf[:], reg("cf"), "pat", 16, 32, "pl", 0, 9, 2.0)

    def ways(i):
        dst = T.cores[rank ^ STEP[i]]
        rl = relays(topo, core, dst)
        return rl, [topo.addr(k, core) for k in rl], [len(topo.engines(k, core)) for k in relays(topo, dst, core)]

    def send(i, land, view, r, k=0):
        rl, ids, _ = ways(i)
        sync("gp", [r], [])
        g.remote_dma(T[land][:], view, remote_sem=T.sem[land], local_sem=T.sem.out, pid=ids[k][1], routing_id=ids[k][0],
                     dma_engine_mask=topo.mask(core, rl[k]))
        outs[0] += len(topo.engines(core, rl[k]))

    def send_two(i, land, pairs, r, k):
        rl, ids, _ = ways(i)
        em = halves(topo, core, rl[k:k + 2])
        sync("gp", [r], [])
        g.remote_dma_fused([
            RemoteDMATransfer(dst_ids=[DstId(rid=ids[k + j][0], pnc=ids[k + j][1])], dma_engine_mask=bits(em[j]),
                              remote_sem=T.sem[land], src=pairs[j][0], dst=pairs[j][1]) for j in range(2)], local_sem=T.sem.out)
        outs[0] += len(em[0]) + len(em[1])

    def places(t):
        iota(T[t][:], [[1, AW]], -MID, 0, reg(t), True)

    def far_ends(t, k):
        cp("ve", T[t][:, k:C:2], T.idt[:, C:AW:2], [reg("idt")], [reg(t, 0, C, k)])

    send_two(0, "mp", [(T.mli[:, a:a + 9], T.mp[:, a:a + 9]) for a in (0, 9)], reg("mli"), 0)

    def unit(b):
        op("ve", lambda e: e.quantize_mx(T.qe[:, 128 * b:128 * b + 128], T.se[:, 128 * b:128 * b + 128], T.et[:, 3 - b:515 - b]),
           [reg("et")], [reg("qe", 128 * b, 128 * b + 128), reg("se", 128 * b, 128 * b + 128)])

    def turn_list(lo, view, r, s1, s2, o0, o1):
        ts(T.lt[:, lo:18:2], view, s1, s2, o0, o1, [r], [reg("lt", 0, 18, lo)])

    def mates_mod():
        ts(T.mt[:], T.lt[:, 0:18], float(H), float(-C), A.is_ge, A.mult, [reg("lt")], [reg("mt")])
        ts(T.mu[:], T.lt[:, 0:18], 2.0, T.c0[:], A.mult, A.add, [reg("lt"), reg("c0")], [reg("mu")])
        tt(T.ct[:, 15:C:16], T.mt[:], T.mu[:], A.add, [reg("mt"), reg("mu")], [reg("ct")])

    cp("ve", T.uo[:], T.idt[:, MID:MID + 128:16], [reg("idt")], [reg("uo")], bias=0.0)
    op("ve", lambda e: e.quantize_mx(T.qu[:], T.su[:], T.ut[:]), [reg("ut")], [reg("qu"), reg("su")])
    for lo in (0, 1):
        turn_list(lo, T.mli[:, 9 * lo:9 * lo + 9], reg("mli"), 0.0, None, A.add, None)
    op("ve", lambda e: e.tensor_copy(T.qr[:, 0:128].bitcast(dt.uint32), T.qu[:, 0:128].bitcast(dt.uint32).indirect(T.uo[:, 0:8])),
       [reg("qu"), reg("uo")], [reg("qr")])
    cp("ac", T.sr[:, 0:128], T.su[:, 0:128].indirect(T.uo[:, 0:8]), [reg("su"), reg("uo")], [reg("sr")])

    def plane(k, lo, b):
        cp("ac", T.xp[:, C * b + lo:C * b + C:2], T["x%d" % k][:, 4 * H * lo + b:4 * H * (lo + 1):4],
           [reg("x%d" % k, H * lo, H * lo + H, b)], [reg("xp", C * b, C * b + C, lo)])

    def state_half(k, lo):
        a = H * lo
        quant("qx", "sx", a, a + H, "x%d" % k, a, a + H)
        if k < ROUNDS:
            mul(lo, "r", 0, "x", a, a + H)
            if lo:
                early = 4 if k else 2
                for b in range(early):
                    plane(k, 1, b)
                cp("ac", T.scl[:], pv(1), [bank(1)], [reg("scl")])
                for b in range(early, 4):
                    plane(k, 1, b)
            else:
                plane(k, 0, 0)
                plane(k, 0, 1)
        else:
            dma("sy", T.oc[:, 4 * a:4 * a + 4 * H], T.qx[:, a:a + H].bitcast(dt.uint8), [reg("qx", a, a + H)], [], "stc%d" % lo)
            mul(lo, "v", 0, "x", a, a + H)
            cp("ac", T.ys[:, a:a + H], pv(lo), [bank(lo)], [reg("ys", a, a + H)])
            dma("ac", T.y[:, a:a + H], T.ys[:, a:a + H], [reg("ys", a, a + H)], [], "sty%d" % lo)

    state_half(0, 1)
    cp("ve", T.cu[:], T.cf[:], [reg("cf")], [reg("cu")])
    mates_mod()
    state_half(0, 0)
    ts(T.cu[:, 15:H:16], T.idt[:, MID:MID + C:32], T.c1[:], None, A.add, None, [reg("idt"), reg("c1")], [reg("cu")])
    cp("ve", T.ta[:], T.idt[:], [reg("idt")], [reg("ta")])

    for i, s in enumerate(STEP):
        x, xn, na, lp = "x%d" % i, "x%d" % (i + 1), "na%d" % i, "lp%d" % i
        qa, qp = "a%d" % i, "p%d" % i
        n_in = ways(i)[2]
        if i == 0:
            arrive("mp", n_in[0] + n_in[1], [reg("mp")])
            arrive("tp", n_in[0], [reg("tp")])
        arrive(lp, n_in[list_relay(i)], [reg(lp)])
        arrive("s" + qp, n_in[0], [reg("s" + qp)])
        arrive("q" + qp, n_in[1] + n_in[2], [reg("q" + qp)])

        tt(T.fl[:, 0:H], pv(0), T.scl[:], A.is_gt, [reg("scl"), bank(0)], [reg("fl", 0, H)])
        tt(T.fl[:, H:C], pv(0), T.scl[:], A.is_le, [reg("scl"), bank(0)], [reg("fl", H, C)])
        if i == 0:
            pick("sc", 0, T.fl[:, 0:H], reg("fl", 0, H), "cu", H, 0.0)
        for a in (0, H):
            pick("scf", a, T.fl[:, a:a + H], reg("fl", a, a + H), "cf", H, 0.0)
        if i == 0:
            cp("ve", T.t0[:, 0:9], T.sc[:, 15:H:16], [reg("sc")], [reg("t0")], bias=float(C))
            send(0, "tp", T.t0[:], reg("t0"))
        for q, k0, k1 in (("ac", 0, 10), ("ve", 10, 18)):
            gather(q, T.gt[:, 16 * k0:16 * k1], reg("gt", 16 * k0, 16 * k1), "fl", 0, C, "lt", k0, k1 - k0, bias=float(OFF))
        plane(i, 0, 2)
        plane(i, 0, 3)
        ts(T.cs[:, 0:36:2], T.scf[:, 15:C:16], -2.0 * C, float(-C), A.mult, A.add, [reg("scf")], [reg("cs", 0, 36, 0)])
        ts(T.cs[:, 1:36:2], T.scf[:, 15:C:16], float(C), float(-C), A.mult, A.add, [reg("scf")], [reg("cs", 0, 36, 1)])
        pick("sct", 0, T.gt[:], reg("gt"), "ct", C, 0.0)
        if i == 0:
            far_ends("up", 1)
            far_ends("upx", 0)
        for lo in (0, 1):
            op("ve", lambda e: e.tensor_tensor_scan(T.nn[:, 20 * lo:20 * lo + 18], T.sct[:, 15:C:16], T.cs[:, 18 * lo:18 * lo + 18],
                                                    float(-C - TW), A.max, A.add),
               [reg("sct"), reg("cs")], [reg("nn", 20 * lo, 20 * lo + 18)])
        if i == 0:
            far_ends("vtab", 1)
        cp("ve", T[na][:], T.nn[:, 1:40:2], [reg("nn")], [reg(na)], bias=float(C + TW))
        send(i, lp, T[na][:], reg(na), list_relay(i))
        if i == 0:
            places("tb")
            places("tc")
            gather("ac", T.cg[:], reg("cg"), "pat", 32, 48, "pl", 0, 9, float(BIG))
            unit(2)

        for b in range(4):
            gather("ac", T.zg[:, b:4 * H:4], reg("zg", 0, H, b), "xp", C * b, C * b + C, na, 0)
        for b in range(4):
            tt(T.z[:, 4 * H + b:4 * C:4], T.xp[:, C * b:C * b + C].indirect(T[na][:, 10:19]), T[x][:, 4 * H + b:4 * C:4], A.add,
               [reg(x, H, C, b), reg("xp", C * b, C * b + C), reg(na, 10, 19)], [reg("z", H, C, b)])
        if i == 0:
            unit(3)
        quant("qz", "sz", H, C, "z", H, C)
        for b in range(4):
            mul(b, "w", 128 * b, "z", H, C)
        part("ac", "up", 0, 2, "idt", C, na, 10, 0, 9)
        if i == 0:
            part("ac", "upx", 1, 2, "idt", C, na, 10, 0, 9)

        def a_copy(q, lo, b):
            k = b if lo else 4 + b
            cp(q, T.a[:, 4 * H * lo + b:4 * H * (lo + 1):4], pv(k), [bank(k)], [reg("a", H * lo, H * lo + H, b)], 0.015625)

        def add_upper(out, got, k):
            a, b = k * H // 2, (k + 1) * H // 2
            tt(T[out][:, 4 * a:4 * b], T[got][:, 4 * a:4 * b], T[x][:, 4 * a:4 * b], A.add, [reg(got, a, b), reg(x, a, b)],
               [reg(out, a, b)])

        a_copy("ac", 1, 0)
        a_copy("ac", 1, 2)
        add_upper("z", "zg", 0)
        add_upper("z", "zg", 1)
        a_copy("ve", 1, 1)
        quant("qz", "sz", 0, H, "z", 0, H)
        a_copy("ve", 1, 3)
        for b in range(4):
            mul(4 + b, "w", 128 * b, "z", 0, H)
        if i == 0:
            for lo in (0, 1):
                cp("ve", T.m0[:, 10 * lo:10 * lo + 9], T.mp[:, 9 * lo:9 * lo + 9], [reg("mp")], [reg("m0", 10 * lo, 10 * lo + 9)])
        quant("q" + qa, "s" + qa, H, C, "a", H, C)
        send_two(i, "q" + qp, [(code_half(T, "q" + qa, H, k), code_half(T, "q" + qp, 0, k)) for k in range(2)],
                 reg("q" + qa, H, C), 1)
        send(i, "s" + qp, T["s" + qa][:, H:C], reg("s" + qa, H, C))
        if i == 0:
            part("ac", "g1", 0, 1, "up", C, "tp", 0, 0, 9)
            part("ve", "g1", H, 1, "upx", C, "tp", 0, 0, 9)
            unit(0)
            a_copy("ac", 0, 0)
            part("ac", "g2", 0, 2, "g1", C, "m0", 0, 0, 9)
            part("ve", "g2", 1, 2, "g1", C, "m0", 10, 0, 9)
            unit(1)
        if i == 1:
            op("ve", lambda e: e.quantize_mx(T.qv[:], T.sv[:], T.vt[:]), [reg("vt")], [reg("qv"), reg("sv")])
        for b in range(0 if i else 1, 4):
            a_copy("ac", 0, b)

        def d_copy(q, lo, b):
            k = 4 + b if lo else b
            cp(q, T.db[:, C * b + H * lo:C * b + H * lo + H], pv(k), [bank(k)], [reg("db", C * b + H * lo, C * b + H * lo + H)])

        def own_d():
            quant("q" + qa, "s" + qa, 0, H, "a", 0, H)
            for b in range(4):
                mul(b, "e", 128 * b, qa, 0, H)
            for b in range(4):
                mul(4 + b, "e", 128 * b, qp, 0, H)

        def to_list(out, o, t, a, step=1, half=None):
            ts(T[out][:, o:o + 9 * step - step + 1:step], T[t][:, a + 15:a + H:16], float(LOW), half, A.add,
               None if half is None else A.mult, [reg(t, a, a + H)],
               [reg(out, o, o + 9) if step == 1 else reg(out, 0, 18, o)])

        spare = [None, None, own_d,
                 lambda: part("ve", "fs", 0, 1, "tb", AW, na, 0, 0, CUT), lambda: part("ve", "fs", 0, 1, "tb", AW, na, 0, CUT, 9),
                 lambda: part("ve", "vtab", 0, 2, "tb", AW, na, 10, 0, CUT),
                 lambda: part("ve", "vtab", 0, 2, "tb", AW, na, 10, CUT, 9), lambda: d_copy("ve", 0, 0), lambda: d_copy("ve", 0, 1),
                 lambda: part("ve", "fs", H, 1, "vtab", C, lp, 10, 0, CUT), lambda: part("ve", "fs", H, 1, "vtab", C, lp, 10, CUT, 9),
                 lambda: d_copy("ve", 0, 2),
                 lambda: [pick("scs", a, T.fs[:, a:a + H], reg("fs", a, a + H), "cg", H, float(-LOW)) for a in (0, H)],
                 lambda: [to_list("ls", o, "scs", a) for o, a in ((0, 0), (10, H))], lambda: d_copy("ve", 0, 3),
                 None]

        def gap():
            f = spare.pop(0)
            if f is not None:
                f()

        def shared(t, win, lk):
            part("ac", t, 1, 2, win, AW, lk, 0, 0, CUT)
            part("ve", t, 1, 2, win, AW, lk, 0, CUT, 9)

        def listed(t, lk):
            gap()
            pick("sc", 0, T[t][:, 1:C:2], reg(t, 0, C, 1), "cg", H, float(-LOW))
            gap()
            to_list(lk, 0, "sc", 0)
            gap()

        part("ve", "ta", 1, 2, "up" if i else "g2", C, lp if i else "tp", 0, 0, 9)
        listed("ta", "lk0")
        if i == 0:
            dma("sy", T.vt[:], T.v[:], [reg("g2")], [reg("vt")], "ldv")
        now, lk = "ta", 0
        for t, more in (("tb", "tc"), ("ta", "tc"), ("ta", "tb"), ("tc", "ta")):
            shared(t, now, "lk%d" % lk)
            part("ac", more, 1, 2, t, AW, "lk%d" % lk, 0, 0, 9)
            now, lk = more, 1 - lk
            listed(t, "lk%d" % lk)
        shared("tb", now, "lk%d" % lk)
        gap()
        part("ve", "fr", 0, 1, "tb", AW, "ls", 0, 0, 9)
        part("ac", "fr", H, 1, "tb", AW, "ls", 10, 0, 9)
        for b in range(2):
            d_copy("ac", 1, b)
        d_copy("ve", 1, 2)
        for a in (0, H):
            pick("scg", a, T.fr[:, a:a + H], reg("fr", a, a + H), "cg", H, float(-LOW))
        for o, a in ((0, 0), (10, H)):
            to_list("lm", o, "scg", a, half=0.5)
        d_copy("ve", 1, 3)
        for b in range(4):
            gather("ac", T.dg[:, b:4 * H:4], reg("dg", 0, H, b), "db", C * b, C * b + C, "lm", 0)
        for b in range(4):
            tt(T[xn][:, 4 * H + b:4 * C:4], T.db[:, C * b:C * b + C].indirect(T.lm[:, 10:19]), T[x][:, 4 * H + b:4 * C:4], A.add,
               [reg("db", C * b, C * b + C), reg("lm", 10, 19), reg(x, H, C, b)], [reg(xn, H, C, b)])
        last = i + 1 == ROUNDS
        if last:
            cp("ac", T.mrow[:], T.fr[:], [reg("fr")], [reg("mrow")], 0.5, float(MID // 2))
            dma("sy", T.mo[:], T.mrow[0:128:16, :], [reg("mrow")], [], "stm")

        def add_plane(b):
            tt(T[xn][:, b:4 * H:4], T.dg[:, b:4 * H:4], T[x][:, b:4 * H:4], A.add, [reg("dg", 0, H, b), reg(x, 0, H, b)],
               [reg(xn, 0, H, b)])
        early = 1 if last else 3
        for b in range(early):
            add_plane(b)
        state_half(i + 1, 1)
        for b in range(early, 4):
            add_plane(b)
        if not last:
            for lo in (0, 1):
                to_list("lt", lo, "scg", H * lo, 2, 0.5)
        state_half(i + 1, 0)
        if not last:
            mates_mod()
    for k in range(4):
        dma("sy", T.osc[4 * k:4 * k + 4, :], T.sx[32 * k:32 * k + 4, :], [reg("sx")], [], "sts%d" % k)
    for n in ("ve", "ac", "pe", "gp"):
        g.wait_ge(T.sem[n], count[n])
    for n in LOADS + STORES:
        g.wait_ge(T.sem[n], 16)
    g.wait_ge(T.sem.out, outs[0])
